import numpy as np
import ml_dtypes


def mxq(x, axis, fmt="e4m3"):
    dtype, down = {"e4m3": (ml_dtypes.float8_e4m3fn, 7), "e5m2": (ml_dtypes.float8_e5m2, 14)}[fmt]
    v = np.moveaxis(np.asarray(x, np.float32).astype(ml_dtypes.bfloat16).astype(np.float64), axis, -1)
    blocks = v.reshape(v.shape[:-1] + (-1, 32))
    amax = np.abs(blocks).max(-1, keepdims=True)
    byte = np.maximum(np.where(amax > 0, np.frexp(amax)[1] - 1 + 127, 0) - down, 1)
    scale = np.exp2(byte - 127.0)
    codes = (blocks / scale).astype(np.float32).astype(dtype).astype(np.float64)
    return np.moveaxis((codes * scale).reshape(v.shape), -1, axis)


WIDE = False


def mx_kscale(k):
    if not WIDE:
        return np.ones(k)
    levels = np.array([10, -10, 5, -5, 0])
    if k % 512:
        return np.exp2(np.random.permutation(np.resize(levels, k // 32))).repeat(32)
    a = np.empty((k // 512, 16))
    for p in range(k // 512):
        a[p, :8] = np.random.permutation(np.resize(levels, 8))
        for g in range(8):
            far = levels[np.abs(levels - a[p, g]) >= 10]
            a[p, g + 8] = far[np.random.randint(len(far))]
    return np.exp2(a.ravel()).repeat(32)


def f64(x):
    return np.asarray(x).astype(np.float64)


def striped(idx):
    return np.tile(idx.reshape(-1, 16).T, (8, 1)).astype(np.uint16)


def unstriped(offs):
    return offs[:16].T.reshape(-1).astype(np.int64)


def striped8(idx):
    return np.concatenate([x.reshape(-1, 16).T for x in idx]).astype(np.uint16)


def runs(offs, k):
    lists = np.stack([offs[16 * r : 16 * r + 16].T.reshape(-1) for r in range(8)]).astype(np.int64)
    return lists[np.arange(k) % 512 // 64]


def pack_weight(w):
    k, n = w.shape
    w = f64(np.asarray(w, np.float32).astype(ml_dtypes.bfloat16)).reshape(k // 32, 32, n)
    amax = np.abs(w).max(1)
    byte = np.clip(np.where(amax > 0, np.frexp(amax)[1] - 1 + 127 - 7, 1), 1, 254)
    scaled = (w * np.exp2(127.0 - byte)[:, None, :]).reshape(k, n).astype(np.float32)
    words = np.ascontiguousarray(scaled.reshape(k // 512, 128, 4, n).transpose(0, 1, 3, 2)).astype(ml_dtypes.float8_e4m3fn).view(np.uint8)
    return words, np.ascontiguousarray(byte.astype(np.uint8).reshape(k // 512, 16, n))


def unpack_weight(words, scales):
    g, p, n, _ = words.shape
    vals = np.ascontiguousarray(words).view(ml_dtypes.float8_e4m3fn).astype(np.float64) * np.repeat(np.exp2(scales.astype(np.float64) - 127.0), 8, axis=1)[..., None]
    return vals.transpose(0, 1, 3, 2).reshape(g * 512, n)


K, T, S, N = 512, 2048, 512, 512


def setup_inputs():
    n = np.random.standard_normal
    s = mx_kscale(K)[:, None]
    packed_xT = pack_weight(n((K, T)) * s)
    return {
        "x_words": packed_xT[0],
        "x_scales": packed_xT[1],
        "w1": (n((K, N)) / np.sqrt(K) / s).astype(np.float32),
        "w2": (n((K, N)) / np.sqrt(K) / s).astype(np.float32),
        "offs": striped(np.random.permutation(T)[:S]),
        "ref": striped(np.random.permutation(T)[:S]),
        "c1": striped8(np.stack([np.random.permutation(S) for _ in range(8)])),
        "c2": striped8(np.stack([np.random.permutation(S) for _ in range(8)])),
        "c3": striped8(np.stack([np.random.permutation(S) for _ in range(8)])),
    }


def reference(x_words, x_scales, w1, w2, offs, ref, c1, c2, c3):
    xq = unpack_weight(x_words, x_scales)[:, unstriped(offs)]
    y = mxq(f64(w1), 0, "e4m3").T @ xq
    x_ref = unpack_weight(x_words, x_scales)[:, unstriped(ref)]
    e = mxq(f64(w2), 0, "e4m3").T @ x_ref
    e2 = np.exp(0.25 * (y * (e[np.arange(N)[:, None], runs(c2, N)])))
    e3 = np.exp(0.25 * (y * (e[np.arange(N)[:, None], runs(c3, N)])))
    e1 = np.exp(0.25 * (y * (e[np.arange(N)[:, None], runs(c1, N)])))
    return (e2 + 2.0 * e3) / (e1 + e2 + e3)

@@ -1,0 +1,156 @@
+from contextlib import ExitStack
+
+import concourse.mybir as mybir
+
+K, T, S, N = 512, 2048, 512, 512
+FLOPS = 2 * 2 * K * N * S
+
+F32 = mybir.dt.float32
+BF16 = mybir.dt.bfloat16
+I32 = mybir.dt.int32
+U32 = mybir.dt.uint32
+U16 = mybir.dt.uint16
+U8 = mybir.dt.uint8
+FP8X4 = mybir.dt.float8_e4m3fn_x4
+ALU = mybir.AluOpType
+ACT = mybir.ActivationFunctionType
+
+P = 128
+PACK = 4
+TILES = N // P
+WINDOW = 2 * S
+
+
+def tile_picked_softarg_none_p_kernel(
+    tc, x_words, x_scales, w1, w2, offs, ref, c1, c2, c3, out
+):
+    nc = tc.nc
+    with ExitStack() as ctx:
+        lists = ctx.enter_context(tc.tile_pool(name="lists", bufs=1))
+        keep = ctx.enter_context(tc.tile_pool(name="keep", bufs=1))
+        work = ctx.enter_context(tc.tile_pool(name="work", bufs=2))
+        psum = ctx.enter_context(tc.psum_pool(name="psum", bufs=1))
+
+        def load_list(name, dram):
+            tile = lists.tile([P, S // 16], U16, name=name)
+            nc.sync.dma_start(tile[:], dram)
+            return tile
+
+        def load_weight_half(name, w, half):
+            tile = keep.tile([P, PACK, N // 2], F32, name=name)
+            cols = slice(half * N // 2, (half + 1) * N // 2)
+            nc.sync.dma_start(tile[:], w.rearrange("(p j) c -> p j c", j=PACK)[:, :, cols])
+            return tile
+
+        table_scales = keep.tile([P, T], U8, name="table_scales")
+        nc.vector.memset(table_scales[:].bitcast(I32), 0)
+        ref_list = load_list("ref_list", ref)
+        table_words = keep.tile([P, T], U32, name="table_words")
+        nc.sync.dma_start(
+            table_words[:].bitcast(I32), x_words[0].rearrange("p n t -> p (n t)").bitcast(I32)
+        )
+        for q in range(4):
+            nc.scalar.dma_start(
+                table_scales[32 * q : 32 * q + 4, :].bitcast(I32),
+                x_scales[0, 4 * q : 4 * q + 4, :].bitcast(I32),
+            )
+        offs_list = load_list("offs_list", offs)
+        w2_raw = [load_weight_half("w2_raw%d" % h, w2, h) for h in range(2)]
+        c1_list = load_list("c1_list", c1)
+        c3_list = load_list("c3_list", c3)
+        c2_list = load_list("c2_list", c2)
+        w1_raw = [load_weight_half("w1_raw%d" % h, w1, h) for h in range(2)]
+
+        windows = [keep.tile([P, WINDOW], F32, name="window%d" % t) for t in range(TILES)]
+        for t in range(TILES):
+            nc.gpsimd.memset(windows[t][:, S:], 0.0)
+
+        def pick(name, offsets, scales_tag):
+            words = keep.tile([P, S], U32, name=name + "_words", align_bytes=64)
+            scales = keep.tile([P, S], U8, name=name + "_scales", tag=scales_tag, align_bytes=64)
+            nc.vector.tensor_copy(words[:], table_words[:].indirect(offsets[:]))
+            nc.vector.tensor_copy(scales[:], table_scales[:].indirect(offsets[:]))
+            return words, scales
+
+        def quantise(name, raw):
+            grouped = keep.tile([P, TILES, P, PACK], BF16, name=name + "_grouped", tag=name + "_grouped", align_bytes=64)
+            for h in range(2):
+                nc.scalar.copy(
+                    grouped[:, :, h * P // 2 : (h + 1) * P // 2, :].rearrange("p t m j -> p m j t"),
+                    raw[h][:].rearrange("p j (m t) -> p m j t", t=TILES),
+                )
+            words = keep.tile([P, N], U32, name=name + "_words", align_bytes=64)
+            scales = keep.tile([P, N], U8, name=name + "_scales", align_bytes=64)
+            nc.vector.quantize_mx(
+                out=words[:].bitcast(FP8X4),
+                scales=scales[:],
+                in_=grouped[:].rearrange("p t m j -> p (t m j)"),
+            )
+            return words, scales
+
+        def project(name, weight, picked, t):
+            cols = slice(t * P, (t + 1) * P)
+            acc = psum.tile([P, S], F32, name=name)
+            nc.tensor.matmul_mx(
+                out=acc[:],
+                lhsT=weight[0][:, cols].bitcast(FP8X4),
+                lhsT_scale=weight[1][:, cols],
+                rhs=picked[0][:].bitcast(FP8X4),
+                rhs_scale=picked[1][:],
+                start=True,
+                stop=True,
+            )
+            return acc
+
+        right = pick("right", ref_list, "right_scales")
+        w2_q = quantise("w2", w2_raw)
+        left = pick("left", offs_list, "w2_grouped")
+        e = [project("e%d" % t, w2_q, right, t) for t in range(TILES)]
+        nc.scalar.copy(windows[0][:, :S], e[0][:])
+        w1_q = quantise("w1", w1_raw)
+        for t in range(1, TILES):
+            nc.scalar.copy(windows[t][:, :S], e[t][:])
+        y = [project("y%d" % t, w1_q, left, t) for t in range(TILES)]
+
+        slope = keep.tile([P, TILES, S], F32, name="slope")
+        steep = keep.tile([P, TILES, S], F32, name="steep")
+        middle = keep.tile([P, TILES, S], F32, name="middle")
+        for t in range(TILES):
+            last = t == TILES - 1
+            g1 = work.tile([P, S], F32, name="g1")
+            d31 = keep.tile([P, S], F32, name="d31")
+            d21 = keep.tile([P, S], F32, name="d21", tag="odds")
+            nc.vector.tensor_copy(g1[:], windows[t][:].indirect(c1_list[:]))
+            nc.vector.tensor_tensor(d31[:], windows[t][:].indirect(c3_list[:]), g1[:], ALU.subtract)
+            nc.vector.tensor_tensor(d21[:], windows[t][:].indirect(c2_list[:]), g1[:], ALU.subtract)
+            s31 = work.tile([P, S], F32, name="s31")
+            s21 = work.tile([P, S], F32, name="s21")
+            nc.vector.tensor_tensor(s31[:], d31[:], y[t][:], ALU.mult)
+            nc.vector.tensor_tensor(s21[:], d21[:], y[t][:], ALU.mult)
+            lead = keep.tile([P, S], F32, name="lead", tag="root")
+            nc.vector.scalar_tensor_tensor(lead[:], s31[:], 0.0, s21[:], ALU.max, ALU.subtract)
+            nc.scalar.activation(slope[:, t, :], s31[:], ACT.Tanh, scale=0.125)
+            nc.scalar.activation(steep[:, t, :], slope[:, t, :], ACT.Abs)
+            nc.scalar.activation(middle[:, t, :], lead[:], ACT.Exp, scale=-0.25)
+
+        odds = keep.tile([P, TILES, S], F32, name="odds", tag="odds")
+        for t in range(TILES):
+            nc.vector.scalar_tensor_tensor(
+                odds[:, t, :], steep[:, t, :], 1.0, middle[:, t, :], ALU.add, ALU.mult
+            )
+        root = keep.tile([P, TILES, S], F32, name="root", tag="root")
+        rows = out.rearrange("(p t) j -> p t j", t=TILES)
+        for t in range(TILES):
+            nc.scalar.activation(root[:, t, :], odds[:, t, :], ACT.Abs_reciprocal_sqrt, bias=1.0, scale=0.5)
+            shift = work.tile([P, S], F32, name="shift")
+            if t < 2:
+                half = work.tile([P, S], F32, name="half")
+                nc.vector.tensor_tensor(half[:], slope[:, t, :], root[:, t, :], ALU.mult)
+                nc.vector.tensor_tensor(shift[:], half[:], root[:, t, :], ALU.mult)
+            else:
+                share = work.tile([P, S], F32, name="share")
+                nc.scalar.activation(share[:], root[:, t, :], ACT.Square)
+                nc.vector.tensor_tensor(shift[:], slope[:, t, :], share[:], ALU.mult)
+            result = keep.tile([P, S], F32, name="result%d" % t)
+            nc.vector.tensor_scalar_add(result[:], shift[:], 1.0)
+            nc.sync.dma_start(rows[:, t, :], result[:])

@@ -1,6 +1,7 @@
 from contextlib import ExitStack
 
 import concourse.mybir as mybir
+from concourse.masks import make_identity
 
 K, T, S, N = 512, 2048, 512, 512
 FLOPS = 2 * 2 * K * N * S
@@ -56,41 +57,61 @@ def tile_picked_softarg_none_p_kernel(
             )
         offs_list = load_list("offs_list", offs)
         w2_raw = [load_weight_half("w2_raw%d" % h, w2, h) for h in range(2)]
+        w1_whole = keep.tile([P, PACK, N], F32, name="w1_whole")
+        nc.sync.dma_start(w1_whole[:], w1.rearrange("(p j) c -> p j c", j=PACK))
+        w1_raw = [w1_whole[:, :, h * N // 2 : (h + 1) * N // 2] for h in range(2)]
         c1_list = load_list("c1_list", c1)
         c3_list = load_list("c3_list", c3)
         c2_list = load_list("c2_list", c2)
-        w1_raw = [load_weight_half("w1_raw%d" % h, w1, h) for h in range(2)]
 
         windows = [keep.tile([P, WINDOW], F32, name="window%d" % t) for t in range(TILES)]
         for t in range(TILES):
             nc.gpsimd.memset(windows[t][:, S:], 0.0)
 
-        def pick(name, offsets, scales_tag):
-            words = keep.tile([P, S], U32, name=name + "_words", align_bytes=64)
-            scales = keep.tile([P, S], U8, name=name + "_scales", tag=scales_tag, align_bytes=64)
-            nc.vector.tensor_copy(words[:], table_words[:].indirect(offsets[:]))
-            nc.vector.tensor_copy(scales[:], table_scales[:].indirect(offsets[:]))
-            return words, scales
+        identity = keep.tile([P, P], F32, name="identity")
+        make_identity(nc, identity[:])
 
-        def quantise(name, raw):
-            grouped = keep.tile([P, TILES, P, PACK], BF16, name=name + "_grouped", tag=name + "_grouped", align_bytes=64)
+        def turn(bank, *terms):
+            count = len(terms) * (S // P)
+            for n, (term, b) in enumerate((term, b) for term in terms for b in range(S // P)):
+                cols = slice(b * P, (b + 1) * P)
+                nc.tensor.matmul(
+                    bank[:, cols], term[:, cols], identity[:],
+                    start=n == 0, stop=n == count - 1, is_transpose=True,
+                )
+
+        def pick_words(name, offsets):
+            words = keep.tile([P, S], U32, name=name, align_bytes=64)
+            nc.vector.tensor_copy(words[:], table_words[:].indirect(offsets[:]))
+            return words
+
+        def pick_scales(name, offsets, tag):
+            scales = keep.tile([P, S], U8, name=name, tag=tag, align_bytes=64)
+            nc.vector.tensor_copy(scales[:], table_scales[:].indirect(offsets[:]))
+            return scales
+
+        def interleave(name, raw, tag):
+            grouped = keep.tile([P, TILES, P, PACK], BF16, name=name, tag=tag, align_bytes=64)
             for h in range(2):
                 nc.scalar.copy(
-                    grouped[:, :, h * P // 2 : (h + 1) * P // 2, :].rearrange("p t m j -> p m j t"),
-                    raw[h][:].rearrange("p j (m t) -> p m j t", t=TILES),
+                    grouped[:, :, h * P // 2 : (h + 1) * P // 2, :].rearrange("p t m j -> p m t j"),
+                    raw[h][:].rearrange("p j (m t) -> p m t j", t=TILES),
                 )
-            words = keep.tile([P, N], U32, name=name + "_words", align_bytes=64)
-            scales = keep.tile([P, N], U8, name=name + "_scales", align_bytes=64)
+            return grouped
+
+        def quantise(name, grouped, first, count):
+            words = keep.tile([P, count * P], U32, name=name + "_words", tag=name + "_words", align_bytes=64)
+            scales = keep.tile([P, count * P], U8, name=name + "_scales", align_bytes=64)
             nc.vector.quantize_mx(
                 out=words[:].bitcast(FP8X4),
                 scales=scales[:],
-                in_=grouped[:].rearrange("p t m j -> p (t m j)"),
+                in_=grouped[:, first : first + count].rearrange("p t m j -> p (t m j)"),
             )
-            return words, scales
+            return [(words, scales, slice(i * P, (i + 1) * P)) for i in range(count)]
 
-        def project(name, weight, picked, t):
-            cols = slice(t * P, (t + 1) * P)
-            acc = psum.tile([P, S], F32, name=name)
+        def project(name, weight, picked):
+            cols = weight[2]
+            acc = psum.tile([P, S], F32, name=name, tag=name)
             nc.tensor.matmul_mx(
                 out=acc[:],
                 lhsT=weight[0][:, cols].bitcast(FP8X4),
@@ -102,21 +123,24 @@ def tile_picked_softarg_none_p_kernel(
             )
             return acc
 
-        right = pick("right", ref_list, "right_scales")
-        w2_q = quantise("w2", w2_raw)
-        left = pick("left", offs_list, "w2_grouped")
-        e = [project("e%d" % t, w2_q, right, t) for t in range(TILES)]
+        right_words = pick_words("right_words", ref_list)
+        left_words = pick_words("left_words", offs_list)
+        right = (right_words, pick_scales("right_scales", ref_list, "right_scales"))
+        w2_grouped = interleave("w2_grouped", w2_raw, "w2_grouped")
+        w2_q = quantise("w2_first", w2_grouped, 0, 1)
+        w2_q += quantise("w2_second", w2_grouped, 1, 1) + quantise("w2_rest", w2_grouped, 2, 2)
+        left = (left_words, pick_scales("left_scales", offs_list, "w2_grouped"))
+        e = [project("e%d" % t, w2_q[t], right) for t in range(TILES)]
         nc.scalar.copy(windows[0][:, :S], e[0][:])
-        w1_q = quantise("w1", w1_raw)
+        w1_q = quantise("w1", interleave("w1_grouped", w1_raw, "w2_first_words"), 0, TILES)
         for t in range(1, TILES):
             nc.scalar.copy(windows[t][:, :S], e[t][:])
-        y = [project("y%d" % t, w1_q, left, t) for t in range(TILES)]
+        y = [project("y%d" % t, w1_q[t], left) for t in range(TILES)]
 
         slope = keep.tile([P, TILES, S], F32, name="slope")
         steep = keep.tile([P, TILES, S], F32, name="steep")
-        middle = keep.tile([P, TILES, S], F32, name="middle")
+        middle = []
         for t in range(TILES):
-            last = t == TILES - 1
             g1 = work.tile([P, S], F32, name="g1")
             d31 = keep.tile([P, S], F32, name="d31")
             d21 = keep.tile([P, S], F32, name="d21", tag="odds")
@@ -124,33 +148,56 @@ def tile_picked_softarg_none_p_kernel(
             nc.vector.tensor_tensor(d31[:], windows[t][:].indirect(c3_list[:]), g1[:], ALU.subtract)
             nc.vector.tensor_tensor(d21[:], windows[t][:].indirect(c2_list[:]), g1[:], ALU.subtract)
             s31 = work.tile([P, S], F32, name="s31")
-            s21 = work.tile([P, S], F32, name="s21")
+            s12 = work.tile([P, S], F32, name="s12")
             nc.vector.tensor_tensor(s31[:], d31[:], y[t][:], ALU.mult)
-            nc.vector.tensor_tensor(s21[:], d21[:], y[t][:], ALU.mult)
-            lead = keep.tile([P, S], F32, name="lead", tag="root")
-            nc.vector.scalar_tensor_tensor(lead[:], s31[:], 0.0, s21[:], ALU.max, ALU.subtract)
+            if t < TILES - 1:
+                nc.vector.scalar_tensor_tensor(s12[:], d21[:], -1.0, y[t][:], ALU.mult, ALU.mult)
+                rise = work.tile([P, S], F32, name="rise")
+                nc.scalar.activation(rise[:], s31[:], ACT.Relu)
             nc.scalar.activation(slope[:, t, :], s31[:], ACT.Tanh, scale=0.125)
             nc.scalar.activation(steep[:, t, :], slope[:, t, :], ACT.Abs)
-            nc.scalar.activation(middle[:, t, :], lead[:], ACT.Exp, scale=-0.25)
+            if t < TILES - 1:
+                lead_turned = psum.tile([P, S], F32, name="lead_turned%d" % t, tag="e%d" % t)
+                turn(lead_turned, rise, s12)
+                middle_turned = work.tile([P, S], F32, name="middle_turned")
+                nc.scalar.activation(middle_turned[:], lead_turned[:], ACT.Exp, scale=-0.25)
+                middle.append(psum.tile([P, S], F32, name="middle%d" % t, tag="e%d" % t))
+                turn(middle[t], middle_turned)
+            else:
+                lead = keep.tile([P, S], F32, name="lead", tag="root")
+                middle.append(keep.tile([P, S], F32, name="middle%d" % t))
+                halves = [slice(h * S // 2, (h + 1) * S // 2) for h in range(2)]
+                for cols in halves:
+                    nc.vector.scalar_tensor_tensor(
+                        s12[:, cols], d21[:, cols], -1.0, y[t][:, cols], ALU.mult, ALU.mult
+                    )
+                for cols in halves:
+                    nc.vector.scalar_tensor_tensor(
+                        lead[:, cols], s31[:, cols], 0.0, s12[:, cols], ALU.max, ALU.add
+                    )
+                    nc.scalar.activation(middle[t][:, cols], lead[:, cols], ACT.Exp, scale=-0.25)
 
         odds = keep.tile([P, TILES, S], F32, name="odds", tag="odds")
         for t in range(TILES):
             nc.vector.scalar_tensor_tensor(
-                odds[:, t, :], steep[:, t, :], 1.0, middle[:, t, :], ALU.add, ALU.mult
+                odds[:, t, :], steep[:, t, :], 1.0, middle[t][:], ALU.add, ALU.mult
             )
         root = keep.tile([P, TILES, S], F32, name="root", tag="root")
         rows = out.rearrange("(p t) j -> p t j", t=TILES)
-        for t in range(TILES):
-            nc.scalar.activation(root[:, t, :], odds[:, t, :], ACT.Abs_reciprocal_sqrt, bias=1.0, scale=0.5)
-            shift = work.tile([P, S], F32, name="shift")
-            if t < 2:
-                half = work.tile([P, S], F32, name="half")
-                nc.vector.tensor_tensor(half[:], slope[:, t, :], root[:, t, :], ALU.mult)
-                nc.vector.tensor_tensor(shift[:], half[:], root[:, t, :], ALU.mult)
+        pieces = [(t, slice(0, S)) for t in range(TILES - 1)]
+        pieces += [(TILES - 1, slice(h * S // 2, (h + 1) * S // 2)) for h in range(2)]
+        for n, (t, cols) in enumerate(pieces):
+            width = cols.stop - cols.start
+            nc.scalar.activation(root[:, t, cols], odds[:, t, cols], ACT.Abs_reciprocal_sqrt, bias=1.0, scale=0.5)
+            shift = work.tile([P, width], F32, name="shift")
+            if t == 0:
+                half = work.tile([P, width], F32, name="half")
+                nc.vector.tensor_tensor(half[:], slope[:, t, cols], root[:, t, cols], ALU.mult)
+                nc.vector.tensor_tensor(shift[:], half[:], root[:, t, cols], ALU.mult)
             else:
-                share = work.tile([P, S], F32, name="share")
-                nc.scalar.activation(share[:], root[:, t, :], ACT.Square)
-                nc.vector.tensor_tensor(shift[:], slope[:, t, :], share[:], ALU.mult)
-            result = keep.tile([P, S], F32, name="result%d" % t)
+                share = work.tile([P, width], F32, name="share")
+                nc.scalar.activation(share[:], root[:, t, cols], ACT.Square)
+                nc.vector.tensor_tensor(shift[:], slope[:, t, cols], share[:], ALU.mult)
+            result = keep.tile([P, width], F32, name="result%d" % n)
             nc.vector.tensor_scalar_add(result[:], shift[:], 1.0)
-            nc.sync.dma_start(rows[:, t, :], result[:])
+            nc.sync.dma_start(rows[:, t, cols], result[:])

@@ -50,12 +50,12 @@ def tile_picked_softarg_none_p_kernel(
         nc.sync.dma_start(
             table_words[:].bitcast(I32), x_words[0].rearrange("p n t -> p (n t)").bitcast(I32)
         )
+        offs_list = load_list("offs_list", offs)
         for q in range(4):
-            nc.scalar.dma_start(
+            nc.sync.dma_start(
                 table_scales[32 * q : 32 * q + 4, :].bitcast(I32),
                 x_scales[0, 4 * q : 4 * q + 4, :].bitcast(I32),
             )
-        offs_list = load_list("offs_list", offs)
         w2_raw = [load_weight_half("w2_raw%d" % h, w2, h) for h in range(2)]
         w1_whole = keep.tile([P, PACK, N], F32, name="w1_whole")
         nc.sync.dma_start(w1_whole[:], w1.rearrange("(p j) c -> p j c", j=PACK))
@@ -66,7 +66,7 @@ def tile_picked_softarg_none_p_kernel(
 
         windows = [keep.tile([P, WINDOW], F32, name="window%d" % t) for t in range(TILES)]
         for t in range(TILES):
-            nc.gpsimd.memset(windows[t][:, S:], 0.0)
+            nc.vector.memset(windows[t][:, S:], 0.0)
 
         identity = keep.tile([P, P], F32, name="identity")
         make_identity(nc, identity[:])
@@ -137,28 +137,51 @@ def tile_picked_softarg_none_p_kernel(
             nc.scalar.copy(windows[t][:, :S], e[t][:])
         y = [project("y%d" % t, w1_q[t], left) for t in range(TILES)]
 
-        slope = keep.tile([P, TILES, S], F32, name="slope")
-        steep = keep.tile([P, TILES, S], F32, name="steep")
+        halves = [slice(h * S // 2, (h + 1) * S // 2) for h in range(2)]
+        last = TILES - 1
+        signed_y = {}
+        for t in range(1, last):
+            plus_y = keep.tile([P, S], F32, name="plus_y%d" % t)
+            minus_y = keep.tile([P, S], F32, name="minus_y%d" % t)
+            nc.scalar.copy(plus_y[:], y[t][:])
+            nc.scalar.activation(minus_y[:], y[t][:], ACT.Copy, scale=-1.0)
+            signed_y[t] = (plus_y, minus_y)
+        slope = []
+        steep = [keep.tile([P, S], F32, name="steep%d" % t) for t in range(TILES)]
         middle = []
         for t in range(TILES):
-            g1 = work.tile([P, S], F32, name="g1")
-            d31 = keep.tile([P, S], F32, name="d31")
-            d21 = keep.tile([P, S], F32, name="d21", tag="odds")
-            nc.vector.tensor_copy(g1[:], windows[t][:].indirect(c1_list[:]))
-            nc.vector.tensor_tensor(d31[:], windows[t][:].indirect(c3_list[:]), g1[:], ALU.subtract)
-            nc.vector.tensor_tensor(d21[:], windows[t][:].indirect(c2_list[:]), g1[:], ALU.subtract)
-            s31 = work.tile([P, S], F32, name="s31")
-            s12 = work.tile([P, S], F32, name="s12")
-            nc.vector.tensor_tensor(s31[:], d31[:], y[t][:], ALU.mult)
-            if t < TILES - 1:
-                nc.vector.scalar_tensor_tensor(s12[:], d21[:], -1.0, y[t][:], ALU.mult, ALU.mult)
-                rise = work.tile([P, S], F32, name="rise")
+            s31 = keep.tile([P, S], F32, name="s31_%d" % t, tag="odds" if t == last else "s31_%d" % t)
+            if t in (0, last):
+                g1 = work.tile([P, S], F32, name="first")
+                d31 = keep.tile([P, S], F32, name="third")
+                d21 = keep.tile([P, S], F32, name="second", tag="w2_first_words" if t == 0 else "minus_s2", align_bytes=64)
+                nc.vector.tensor_copy(g1[:], windows[t][:].indirect(c1_list[:]))
+                nc.vector.tensor_tensor(d31[:], windows[t][:].indirect(c3_list[:]), g1[:], ALU.subtract)
+                nc.vector.tensor_tensor(d21[:], windows[t][:].indirect(c2_list[:]), g1[:], ALU.subtract)
+                nc.vector.tensor_tensor(s31[:], d31[:], y[t][:], ALU.mult)
+                s12 = keep.tile([P, S], F32, name="s12_%d" % t)
+                terms = [s12]
+                if t == 0:
+                    nc.vector.scalar_tensor_tensor(s12[:], d21[:], -1.0, y[t][:], ALU.mult, ALU.mult)
+            else:
+                plus_y, minus_y = signed_y[t]
+                s1 = work.tile([P, S], F32, name="first")
+                s3 = keep.tile([P, S], F32, name="third")
+                minus_s2 = keep.tile([P, S], F32, name="minus_s2_%d" % t, tag="minus_s2", align_bytes=64)
+                nc.vector.tensor_tensor(s1[:], windows[t][:].indirect(c1_list[:]), plus_y[:], ALU.mult)
+                nc.vector.tensor_tensor(s3[:], windows[t][:].indirect(c3_list[:]), plus_y[:], ALU.mult)
+                nc.vector.tensor_tensor(minus_s2[:], windows[t][:].indirect(c2_list[:]), minus_y[:], ALU.mult)
+                nc.vector.tensor_tensor(s31[:], s3[:], s1[:], ALU.subtract)
+                terms = [s1, minus_s2]
+            if t < last:
+                rise = keep.tile([P, S], F32, name="rise%d" % t, tag="odds" if t == last - 1 else "rise%d" % t)
                 nc.scalar.activation(rise[:], s31[:], ACT.Relu)
-            nc.scalar.activation(slope[:, t, :], s31[:], ACT.Tanh, scale=0.125)
-            nc.scalar.activation(steep[:, t, :], slope[:, t, :], ACT.Abs)
-            if t < TILES - 1:
+            slope.append(keep.tile([P, S], F32, name="slope%d" % t))
+            nc.scalar.activation(slope[t][:], s31[:], ACT.Tanh, scale=0.125)
+            nc.scalar.activation(steep[t][:], slope[t][:], ACT.Abs)
+            if t < last:
                 lead_turned = psum.tile([P, S], F32, name="lead_turned%d" % t, tag="e%d" % t)
-                turn(lead_turned, rise, s12)
+                turn(lead_turned, *terms, rise)
                 middle_turned = work.tile([P, S], F32, name="middle_turned")
                 nc.scalar.activation(middle_turned[:], lead_turned[:], ACT.Exp, scale=-0.25)
                 middle.append(psum.tile([P, S], F32, name="middle%d" % t, tag="e%d" % t))
@@ -166,7 +189,6 @@ def tile_picked_softarg_none_p_kernel(
             else:
                 lead = keep.tile([P, S], F32, name="lead", tag="root")
                 middle.append(keep.tile([P, S], F32, name="middle%d" % t))
-                halves = [slice(h * S // 2, (h + 1) * S // 2) for h in range(2)]
                 for cols in halves:
                     nc.vector.scalar_tensor_tensor(
                         s12[:, cols], d21[:, cols], -1.0, y[t][:, cols], ALU.mult, ALU.mult
@@ -179,25 +201,26 @@ def tile_picked_softarg_none_p_kernel(
 
         odds = keep.tile([P, TILES, S], F32, name="odds", tag="odds")
         for t in range(TILES):
-            nc.vector.scalar_tensor_tensor(
-                odds[:, t, :], steep[:, t, :], 1.0, middle[t][:], ALU.add, ALU.mult
-            )
+            nc.vector.scalar_tensor_tensor(odds[:, t, :], steep[t][:], 1.0, middle[t][:], ALU.add, ALU.mult)
         root = keep.tile([P, TILES, S], F32, name="root", tag="root")
         rows = out.rearrange("(p t) j -> p t j", t=TILES)
-        pieces = [(t, slice(0, S)) for t in range(TILES - 1)]
-        pieces += [(TILES - 1, slice(h * S // 2, (h + 1) * S // 2)) for h in range(2)]
+        pieces = [(t, slice(0, S)) for t in range(last)] + [(last, cols) for cols in halves]
+        shifts = []
         for n, (t, cols) in enumerate(pieces):
             width = cols.stop - cols.start
             nc.scalar.activation(root[:, t, cols], odds[:, t, cols], ACT.Abs_reciprocal_sqrt, bias=1.0, scale=0.5)
-            shift = work.tile([P, width], F32, name="shift")
+            shifts.append(keep.tile([P, width], F32, name="shift%d" % n))
+            factor = keep.tile([P, width], F32, name="factor%d" % n)
             if t == 0:
-                half = work.tile([P, width], F32, name="half")
-                nc.vector.tensor_tensor(half[:], slope[:, t, cols], root[:, t, cols], ALU.mult)
-                nc.vector.tensor_tensor(shift[:], half[:], root[:, t, cols], ALU.mult)
+                nc.vector.tensor_tensor(factor[:], slope[t][:, cols], root[:, t, cols], ALU.mult)
+                nc.vector.tensor_tensor(shifts[n][:], factor[:], root[:, t, cols], ALU.mult)
             else:
-                share = work.tile([P, width], F32, name="share")
-                nc.scalar.activation(share[:], root[:, t, cols], ACT.Square)
-                nc.vector.tensor_tensor(shift[:], slope[:, t, cols], share[:], ALU.mult)
-            result = keep.tile([P, width], F32, name="result%d" % n)
-            nc.vector.tensor_scalar_add(result[:], shift[:], 1.0)
-            nc.sync.dma_start(rows[:, t, cols], result[:])
+                nc.scalar.activation(factor[:], root[:, t, cols], ACT.Square)
+                nc.vector.tensor_tensor(shifts[n][:], slope[t][:, cols], factor[:], ALU.mult)
+            if n != last:
+                result = keep.tile([P, width], F32, name="result%d" % n)
+                nc.vector.tensor_scalar_add(result[:], shifts[n][:], 1.0)
+                nc.sync.dma_start(rows[:, t, cols], result[:])
+        result = keep.tile([P, S // 2], F32, name="result%d" % last)
+        nc.scalar.activation(result[:], shifts[last][:], ACT.Identity, bias=1.0)
+        nc.scalar.dma_start(rows[:, last, halves[0]], result[:])

@@ -20,6 +20,7 @@ P = 128
 PACK = 4
 TILES = N // P
 WINDOW = 2 * S
+ADDS_ON_VECTOR = 2
 
 
 def tile_picked_softarg_none_p_kernel(
@@ -29,7 +30,6 @@ def tile_picked_softarg_none_p_kernel(
     with ExitStack() as ctx:
         lists = ctx.enter_context(tc.tile_pool(name="lists", bufs=1))
         keep = ctx.enter_context(tc.tile_pool(name="keep", bufs=1))
-        work = ctx.enter_context(tc.tile_pool(name="work", bufs=2))
         psum = ctx.enter_context(tc.psum_pool(name="psum", bufs=1))
 
         def load_list(name, dram):
@@ -37,70 +37,71 @@ def tile_picked_softarg_none_p_kernel(
             nc.sync.dma_start(tile[:], dram)
             return tile
 
-        def load_weight_half(name, w, half):
-            tile = keep.tile([P, PACK, N // 2], F32, name=name)
-            cols = slice(half * N // 2, (half + 1) * N // 2)
-            nc.sync.dma_start(tile[:], w.rearrange("(p j) c -> p j c", j=PACK)[:, :, cols])
-            return tile
-
         table_scales = keep.tile([P, T], U8, name="table_scales")
-        nc.vector.memset(table_scales[:].bitcast(I32), 0)
+        nc.gpsimd.memset(table_scales[:].bitcast(I32), 0)
         ref_list = load_list("ref_list", ref)
+        for q in range(4):
+            (nc.sync if q < 2 else nc.scalar).dma_start(
+                table_scales[32 * q : 32 * q + 4, :].bitcast(I32),
+                x_scales[0, 4 * q : 4 * q + 4, :].bitcast(I32),
+            )
+        offs_list = load_list("offs_list", offs)
+        w2_whole = keep.tile([P, PACK, N], F32, name="w2_whole")
+        nc.sync.dma_start(w2_whole[:], w2.rearrange("(p j) c -> p j c", j=PACK))
         table_words = keep.tile([P, T], U32, name="table_words")
         nc.sync.dma_start(
             table_words[:].bitcast(I32), x_words[0].rearrange("p n t -> p (n t)").bitcast(I32)
         )
-        offs_list = load_list("offs_list", offs)
-        for q in range(4):
-            nc.sync.dma_start(
-                table_scales[32 * q : 32 * q + 4, :].bitcast(I32),
-                x_scales[0, 4 * q : 4 * q + 4, :].bitcast(I32),
-            )
-        w2_raw = [load_weight_half("w2_raw%d" % h, w2, h) for h in range(2)]
-        w1_whole = keep.tile([P, PACK, N], F32, name="w1_whole")
-        nc.sync.dma_start(w1_whole[:], w1.rearrange("(p j) c -> p j c", j=PACK))
-        w1_raw = [w1_whole[:, :, h * N // 2 : (h + 1) * N // 2] for h in range(2)]
+        windows = [keep.tile([P, WINDOW], F32, name="window%d" % t) for t in range(TILES)]
+        w1_rows = w1.rearrange("(p j) c -> p j c", j=PACK)
+        w1_raw = [windows[h][:].rearrange("p (j c) -> p j c", j=PACK) for h in range(2)]
+        for h in range(2):
+            nc.sync.dma_start(w1_raw[h], w1_rows[:, :, h * N // 2 : (h + 1) * N // 2])
         c1_list = load_list("c1_list", c1)
         c3_list = load_list("c3_list", c3)
         c2_list = load_list("c2_list", c2)
 
-        windows = [keep.tile([P, WINDOW], F32, name="window%d" % t) for t in range(TILES)]
-        for t in range(TILES):
+        for t in (2, 3):
             nc.vector.memset(windows[t][:, S:], 0.0)
 
         identity = keep.tile([P, P], F32, name="identity")
         make_identity(nc, identity[:])
 
-        def turn(bank, *terms):
+        def turn(bank, terms, opens, closes):
             count = len(terms) * (S // P)
             for n, (term, b) in enumerate((term, b) for term in terms for b in range(S // P)):
                 cols = slice(b * P, (b + 1) * P)
                 nc.tensor.matmul(
                     bank[:, cols], term[:, cols], identity[:],
-                    start=n == 0, stop=n == count - 1, is_transpose=True,
+                    start=opens and n == 0, stop=closes and n == count - 1, is_transpose=True,
                 )
 
-        def pick_words(name, offsets):
-            words = keep.tile([P, S], U32, name=name, align_bytes=64)
+        def pick_words(name, offsets, tag):
+            words = keep.tile([P, S], U32, name=name, tag=tag, align_bytes=64)
             nc.vector.tensor_copy(words[:], table_words[:].indirect(offsets[:]))
             return words
 
-        def pick_scales(name, offsets, tag):
-            scales = keep.tile([P, S], U8, name=name, tag=tag, align_bytes=64)
+        def pick_scales(name, offsets):
+            scales = keep.tile([P, S], U8, name=name, align_bytes=64)
             nc.vector.tensor_copy(scales[:], table_scales[:].indirect(offsets[:]))
             return scales
 
-        def interleave(name, raw, tag):
-            grouped = keep.tile([P, TILES, P, PACK], BF16, name=name, tag=tag, align_bytes=64)
-            for h in range(2):
-                nc.scalar.copy(
-                    grouped[:, :, h * P // 2 : (h + 1) * P // 2, :].rearrange("p t m j -> p m t j"),
-                    raw[h][:].rearrange("p j (m t) -> p m t j", t=TILES),
-                )
+        def interleave_pair(name, whole, pair, copy):
+            grouped = keep.tile([P, 2, P, PACK], BF16, name=name, tag=name, align_bytes=64)
+            copy(
+                grouped[:].rearrange("p t m j -> p m t j"),
+                whole[:].rearrange("p j (m t) -> p m t j", t=TILES)[:, :, 2 * pair : 2 * pair + 2, :],
+            )
             return grouped
 
+        def interleave_half(grouped, raw, h):
+            nc.scalar.copy(
+                grouped[:, :, h * P // 2 : (h + 1) * P // 2, :].rearrange("p t m j -> p m t j"),
+                raw.rearrange("p j (m t) -> p m t j", t=TILES),
+            )
+
         def quantise(name, grouped, first, count):
-            words = keep.tile([P, count * P], U32, name=name + "_words", tag=name + "_words", align_bytes=64)
+            words = keep.tile([P, count * P], U32, name=name + "_words", align_bytes=64)
             scales = keep.tile([P, count * P], U8, name=name + "_scales", align_bytes=64)
             nc.vector.quantize_mx(
                 out=words[:].bitcast(FP8X4),
@@ -109,9 +110,9 @@ def tile_picked_softarg_none_p_kernel(
             )
             return [(words, scales, slice(i * P, (i + 1) * P)) for i in range(count)]
 
-        def project(name, weight, picked):
+        def project(name, weight, picked, bank):
             cols = weight[2]
-            acc = psum.tile([P, S], F32, name=name, tag=name)
+            acc = psum.tile([P, S], F32, name=name, tag=bank)
             nc.tensor.matmul_mx(
                 out=acc[:],
                 lhsT=weight[0][:, cols].bitcast(FP8X4),
@@ -123,104 +124,110 @@ def tile_picked_softarg_none_p_kernel(
             )
             return acc
 
-        right_words = pick_words("right_words", ref_list)
-        left_words = pick_words("left_words", offs_list)
-        right = (right_words, pick_scales("right_scales", ref_list, "right_scales"))
-        w2_grouped = interleave("w2_grouped", w2_raw, "w2_grouped")
-        w2_q = quantise("w2_first", w2_grouped, 0, 1)
-        w2_q += quantise("w2_second", w2_grouped, 1, 1) + quantise("w2_rest", w2_grouped, 2, 2)
-        left = (left_words, pick_scales("left_scales", offs_list, "w2_grouped"))
-        e = [project("e%d" % t, w2_q[t], right) for t in range(TILES)]
+        right_scales = pick_scales("right_scales", ref_list)
+        left_scales = pick_scales("left_scales", offs_list)
+        w2_low = interleave_pair("w2_low", w2_whole, 0, nc.vector.tensor_copy)
+        w2_high = interleave_pair("w2_high", w2_whole, 1, nc.scalar.copy)
+        w2_q = quantise("w2_low", w2_low, 0, 2) + quantise("w2_high", w2_high, 0, 2)
+        right = (pick_words("right_words", ref_list, "w2_low"), right_scales)
+        left = (pick_words("left_words", offs_list, "w2_high"), left_scales)
+        e = {t: project("e%d" % t, w2_q[t], right, "e%d" % t) for t in range(2)}
+        w1_grouped = keep.tile([P, TILES, P, PACK], BF16, name="w1_grouped", tag="w1_grouped", align_bytes=64)
+        interleave_half(w1_grouped, w1_raw[0], 0)
         nc.scalar.copy(windows[0][:, :S], e[0][:])
-        w1_q = quantise("w1", interleave("w1_grouped", w1_raw, "w2_first_words"), 0, TILES)
-        for t in range(1, TILES):
-            nc.scalar.copy(windows[t][:, :S], e[t][:])
-        y = [project("y%d" % t, w1_q[t], left) for t in range(TILES)]
+        interleave_half(w1_grouped, w1_raw[1], 1)
+        w1_q = quantise("w1_low", w1_grouped, 0, 2) + quantise("w1_high", w1_grouped, 2, 2)
+        y = {t: project("y%d" % t, w1_q[t], left, "y%d" % t) for t in (1, 0, 2, 3)}
 
         halves = [slice(h * S // 2, (h + 1) * S // 2) for h in range(2)]
         last = TILES - 1
-        signed_y = {}
+        nc.scalar.copy(windows[1][:, :S], e[1][:])
+
+        def scaled_y(name, t, scale, tag):
+            tile = keep.tile([P, S], F32, name="%s%d" % (name, t), tag=tag)
+            nc.scalar.activation(tile[:], y[t][:], ACT.Copy, scale=scale)
+            return tile
+
+        eighth_y = {}
+        minus_y = {}
         for t in range(1, last):
-            plus_y = keep.tile([P, S], F32, name="plus_y%d" % t)
-            minus_y = keep.tile([P, S], F32, name="minus_y%d" % t)
-            nc.scalar.copy(plus_y[:], y[t][:])
-            nc.scalar.activation(minus_y[:], y[t][:], ACT.Copy, scale=-1.0)
-            signed_y[t] = (plus_y, minus_y)
-        slope = []
-        steep = [keep.tile([P, S], F32, name="steep%d" % t) for t in range(TILES)]
-        middle = []
+            eighth_y[t] = scaled_y("eighth_y", t, 0.125, "eighth_y%d" % t)
+            minus_y[t] = scaled_y("minus_y", t, -0.25, "minus_y%d" % t)
+            e[t + 1] = project("e%d" % (t + 1), w2_q[t + 1], right, "y%d" % t)
+        lead_banks = ["e0", "e1", "y1", "y2"]
+        outer_banks = ["outer0", "outer1", "y0", "y3"]
+        lead_turned = []
+        half_gap = []
+        slope = {}
+        small = keep.tile([P, TILES, S], F32, name="small")
         for t in range(TILES):
-            s31 = keep.tile([P, S], F32, name="s31_%d" % t, tag="odds" if t == last else "s31_%d" % t)
-            if t in (0, last):
-                g1 = work.tile([P, S], F32, name="first")
-                d31 = keep.tile([P, S], F32, name="third")
-                d21 = keep.tile([P, S], F32, name="second", tag="w2_first_words" if t == 0 else "minus_s2", align_bytes=64)
+            half_gap.append(keep.tile([P, S], F32, name="half_gap%d" % t))
+            if t == 0:
+                g1 = keep.tile([P, S], F32, name="first0")
+                d31 = keep.tile([P, S], F32, name="third0", tag="w1_grouped", align_bytes=64)
                 nc.vector.tensor_copy(g1[:], windows[t][:].indirect(c1_list[:]))
                 nc.vector.tensor_tensor(d31[:], windows[t][:].indirect(c3_list[:]), g1[:], ALU.subtract)
-                nc.vector.tensor_tensor(d21[:], windows[t][:].indirect(c2_list[:]), g1[:], ALU.subtract)
-                nc.vector.tensor_tensor(s31[:], d31[:], y[t][:], ALU.mult)
-                s12 = keep.tile([P, S], F32, name="s12_%d" % t)
-                terms = [s12]
-                if t == 0:
-                    nc.vector.scalar_tensor_tensor(s12[:], d21[:], -1.0, y[t][:], ALU.mult, ALU.mult)
+                nc.vector.scalar_tensor_tensor(half_gap[t][:], d31[:], 0.125, y[t][:], ALU.mult, ALU.mult)
+                terms = [half_gap[t]]
             else:
-                plus_y, minus_y = signed_y[t]
-                s1 = work.tile([P, S], F32, name="first")
-                s3 = keep.tile([P, S], F32, name="third")
-                minus_s2 = keep.tile([P, S], F32, name="minus_s2_%d" % t, tag="minus_s2", align_bytes=64)
-                nc.vector.tensor_tensor(s1[:], windows[t][:].indirect(c1_list[:]), plus_y[:], ALU.mult)
-                nc.vector.tensor_tensor(s3[:], windows[t][:].indirect(c3_list[:]), plus_y[:], ALU.mult)
-                nc.vector.tensor_tensor(minus_s2[:], windows[t][:].indirect(c2_list[:]), minus_y[:], ALU.mult)
-                nc.vector.tensor_tensor(s31[:], s3[:], s1[:], ALU.subtract)
-                terms = [s1, minus_s2]
+                s1 = keep.tile([P, S], F32, name="first%d" % t)
+                s3 = keep.tile([P, S], F32, name="third%d" % t)
+                nc.vector.tensor_tensor(s1[:], windows[t][:].indirect(c1_list[:]), eighth_y[t][:], ALU.mult)
+                nc.vector.tensor_tensor(s3[:], windows[t][:].indirect(c3_list[:]), eighth_y[t][:], ALU.mult)
+                for cols in [slice(0, S)] if t < last else halves:
+                    nc.vector.tensor_tensor(half_gap[t][:, cols], s3[:, cols], s1[:, cols], ALU.subtract)
+                terms = [s1, s3]
+            if t + 2 < TILES:
+                nc.scalar.copy(windows[t + 2][:, :S], e[t + 2][:])
+            if t == 1:
+                eighth_y[last] = scaled_y("eighth_y", last, 0.125, "second")
+            if t == 2:
+                minus_y[last] = scaled_y("minus_y", last, -0.25, "minus_y3")
+            size = keep.tile([P, S], F32, name="size%d" % t)
+            for cols in [slice(0, S)] if t < last else halves:
+                nc.scalar.activation(size[:, cols], half_gap[t][:, cols], ACT.Abs)
+                nc.scalar.activation(small[:, t, cols], size[:, cols], ACT.Exp, scale=-2.0)
             if t < last:
-                rise = keep.tile([P, S], F32, name="rise%d" % t, tag="odds" if t == last - 1 else "rise%d" % t)
-                nc.scalar.activation(rise[:], s31[:], ACT.Relu)
-            slope.append(keep.tile([P, S], F32, name="slope%d" % t))
-            nc.scalar.activation(slope[t][:], s31[:], ACT.Tanh, scale=0.125)
-            nc.scalar.activation(steep[t][:], slope[t][:], ACT.Abs)
-            if t < last:
-                lead_turned = psum.tile([P, S], F32, name="lead_turned%d" % t, tag="e%d" % t)
-                turn(lead_turned, *terms, rise)
-                middle_turned = work.tile([P, S], F32, name="middle_turned")
-                nc.scalar.activation(middle_turned[:], lead_turned[:], ACT.Exp, scale=-0.25)
-                middle.append(psum.tile([P, S], F32, name="middle%d" % t, tag="e%d" % t))
-                turn(middle[t], middle_turned)
-            else:
-                lead = keep.tile([P, S], F32, name="lead", tag="root")
-                middle.append(keep.tile([P, S], F32, name="middle%d" % t))
-                for cols in halves:
-                    nc.vector.scalar_tensor_tensor(
-                        s12[:, cols], d21[:, cols], -1.0, y[t][:, cols], ALU.mult, ALU.mult
-                    )
-                for cols in halves:
-                    nc.vector.scalar_tensor_tensor(
-                        lead[:, cols], s31[:, cols], 0.0, s12[:, cols], ALU.max, ALU.add
-                    )
-                    nc.scalar.activation(middle[t][:, cols], lead[:, cols], ACT.Exp, scale=-0.25)
+                slope[t] = keep.tile([P, S], F32, name="slope%d" % t)
+                nc.scalar.activation(slope[t][:], half_gap[t][:], ACT.Tanh)
+            lead_turned.append(psum.tile([P, S], F32, name="lead_turned%d" % t, tag=lead_banks[t]))
+            turn(lead_turned[t], terms + [size], True, False)
 
-        odds = keep.tile([P, TILES, S], F32, name="odds", tag="odds")
+        second = keep.tile([P, TILES, S], F32, name="second", tag="second")
+        d21 = keep.tile([P, S], F32, name="d21")
+        nc.vector.tensor_tensor(second[:, 0, :], windows[0][:].indirect(c2_list[:]), g1[:], ALU.subtract)
+        for t in range(1, TILES):
+            nc.vector.tensor_tensor(second[:, t, :], windows[t][:].indirect(c2_list[:]), minus_y[t][:], ALU.mult)
+            if t == 1:
+                nc.vector.scalar_tensor_tensor(d21[:], second[:, 0, :], -0.25, y[0][:], ALU.mult, ALU.mult)
+                turn(lead_turned[0], [d21], False, False)
+            turn(lead_turned[t], [second[:, t, :]], False, False)
+
+        soft = keep.tile([P, TILES, S], F32, name="soft")
+        nc.scalar.activation(
+            soft[:].rearrange("p t j -> p (t j)"), small[:].rearrange("p t j -> p (t j)"), ACT.Ln, bias=1.0
+        )
         for t in range(TILES):
-            nc.vector.scalar_tensor_tensor(odds[:, t, :], steep[t][:], 1.0, middle[t][:], ALU.add, ALU.mult)
-        root = keep.tile([P, TILES, S], F32, name="root", tag="root")
+            turn(lead_turned[t], [soft[:, t, :]], False, True)
+
         rows = out.rearrange("(p t) j -> p t j", t=TILES)
-        pieces = [(t, slice(0, S)) for t in range(last)] + [(last, cols) for cols in halves]
-        shifts = []
-        for n, (t, cols) in enumerate(pieces):
-            width = cols.stop - cols.start
-            nc.scalar.activation(root[:, t, cols], odds[:, t, cols], ACT.Abs_reciprocal_sqrt, bias=1.0, scale=0.5)
-            shifts.append(keep.tile([P, width], F32, name="shift%d" % n))
-            factor = keep.tile([P, width], F32, name="factor%d" % n)
-            if t == 0:
-                nc.vector.tensor_tensor(factor[:], slope[t][:, cols], root[:, t, cols], ALU.mult)
-                nc.vector.tensor_tensor(shifts[n][:], factor[:], root[:, t, cols], ALU.mult)
-            else:
-                nc.scalar.activation(factor[:], root[:, t, cols], ACT.Square)
-                nc.vector.tensor_tensor(shifts[n][:], slope[t][:, cols], factor[:], ALU.mult)
-            if n != last:
-                result = keep.tile([P, width], F32, name="result%d" % n)
-                nc.vector.tensor_scalar_add(result[:], shifts[n][:], 1.0)
-                nc.sync.dma_start(rows[:, t, cols], result[:])
-        result = keep.tile([P, S // 2], F32, name="result%d" % last)
-        nc.scalar.activation(result[:], shifts[last][:], ACT.Identity, bias=1.0)
-        nc.scalar.dma_start(rows[:, last, halves[0]], result[:])
+        outer = []
+        for t in range(TILES):
+            outer_turned = keep.tile([P, S], F32, name="outer_turned%d" % t, tag="outer_turned%d" % t)
+            nc.scalar.activation(outer_turned[:], lead_turned[t][:], ACT.Tanh, scale=0.5)
+            outer.append(psum.tile([P, S], F32, name="outer%d" % t, tag=outer_banks[t]))
+            turn(outer[t], [outer_turned], True, True)
+        slope[last] = keep.tile([P, S], F32, name="slope%d" % last, tag="outer_turned1")
+        nc.scalar.activation(slope[last][:], half_gap[last][:], ACT.Tanh)
+        for t in range(TILES):
+            for n, cols in enumerate([slice(0, S)] if t < last else halves):
+                width = cols.stop - cols.start
+                shift = keep.tile([P, width], F32, name="shift%d_%d" % (t, n))
+                nc.vector.scalar_tensor_tensor(shift[:], outer[t][:, cols], 1.0, slope[t][:, cols], ALU.add, ALU.mult)
+                result = keep.tile([P, width], F32, name="result%d_%d" % (t, n))
+                if t >= ADDS_ON_VECTOR and n == 0:
+                    nc.scalar.activation(result[:], shift[:], ACT.Identity, bias=1.0, scale=0.5)
+                    nc.scalar.dma_start(rows[:, t, cols], result[:])
+                else:
+                    nc.vector.tensor_scalar(result[:], shift[:], 0.5, 1.0, ALU.mult, ALU.add)
+                    nc.sync.dma_start(rows[:, t, cols], result[:])

@@ -20,7 +20,7 @@ P = 128
 PACK = 4
 TILES = N // P
 WINDOW = 2 * S
-ADDS_ON_VECTOR = 2
+PLAIN = 2
 
 
 def tile_picked_softarg_none_p_kernel(
@@ -52,24 +52,24 @@ def tile_picked_softarg_none_p_kernel(
         nc.sync.dma_start(
             table_words[:].bitcast(I32), x_words[0].rearrange("p n t -> p (n t)").bitcast(I32)
         )
-        windows = [keep.tile([P, WINDOW], F32, name="window%d" % t) for t in range(TILES)]
-        w1_rows = w1.rearrange("(p j) c -> p j c", j=PACK)
-        w1_raw = [windows[h][:].rearrange("p (j c) -> p j c", j=PACK) for h in range(2)]
-        for h in range(2):
-            nc.sync.dma_start(w1_raw[h], w1_rows[:, :, h * N // 2 : (h + 1) * N // 2])
         c1_list = load_list("c1_list", c1)
         c3_list = load_list("c3_list", c3)
+        windows = [keep.tile([P, WINDOW], F32, name="window%d" % t) for t in range(TILES)]
+        w1_rows = w1.rearrange("(p j) c -> p j c", j=PACK)
+        w1_raw = [windows[1 + h][:].rearrange("p (j c) -> p j c", j=PACK) for h in range(2)]
+        for h in range(2):
+            nc.sync.dma_start(w1_raw[h], w1_rows[:, :, h * N // 2 : (h + 1) * N // 2])
         c2_list = load_list("c2_list", c2)
 
-        for t in (2, 3):
+        for t in (0, 3):
             nc.vector.memset(windows[t][:, S:], 0.0)
 
         identity = keep.tile([P, P], F32, name="identity")
         make_identity(nc, identity[:])
 
-        def turn(bank, terms, opens, closes):
-            count = len(terms) * (S // P)
-            for n, (term, b) in enumerate((term, b) for term in terms for b in range(S // P)):
+        def turn(bank, terms, opens, closes, width=S):
+            count = len(terms) * (width // P)
+            for n, (term, b) in enumerate((term, b) for term in terms for b in range(width // P)):
                 cols = slice(b * P, (b + 1) * P)
                 nc.tensor.matmul(
                     bank[:, cols], term[:, cols], identity[:],
@@ -110,15 +110,15 @@ def tile_picked_softarg_none_p_kernel(
             )
             return [(words, scales, slice(i * P, (i + 1) * P)) for i in range(count)]
 
-        def project(name, weight, picked, bank):
+        def project(name, weight, picked, bank, tokens=slice(0, S)):
             cols = weight[2]
-            acc = psum.tile([P, S], F32, name=name, tag=bank)
+            acc = psum.tile([P, tokens.stop - tokens.start], F32, name=name, tag=bank)
             nc.tensor.matmul_mx(
                 out=acc[:],
                 lhsT=weight[0][:, cols].bitcast(FP8X4),
                 lhsT_scale=weight[1][:, cols],
-                rhs=picked[0][:].bitcast(FP8X4),
-                rhs_scale=picked[1][:],
+                rhs=picked[0][:, tokens].bitcast(FP8X4),
+                rhs_scale=picked[1][:, tokens],
                 start=True,
                 stop=True,
             )
@@ -129,105 +129,125 @@ def tile_picked_softarg_none_p_kernel(
         w2_low = interleave_pair("w2_low", w2_whole, 0, nc.vector.tensor_copy)
         w2_high = interleave_pair("w2_high", w2_whole, 1, nc.scalar.copy)
         w2_q = quantise("w2_low", w2_low, 0, 2) + quantise("w2_high", w2_high, 0, 2)
-        right = (pick_words("right_words", ref_list, "w2_low"), right_scales)
-        left = (pick_words("left_words", offs_list, "w2_high"), left_scales)
-        e = {t: project("e%d" % t, w2_q[t], right, "e%d" % t) for t in range(2)}
-        w1_grouped = keep.tile([P, TILES, P, PACK], BF16, name="w1_grouped", tag="w1_grouped", align_bytes=64)
-        interleave_half(w1_grouped, w1_raw[0], 0)
-        nc.scalar.copy(windows[0][:, :S], e[0][:])
-        interleave_half(w1_grouped, w1_raw[1], 1)
-        w1_q = quantise("w1_low", w1_grouped, 0, 2) + quantise("w1_high", w1_grouped, 2, 2)
-        y = {t: project("y%d" % t, w1_q[t], left, "y%d" % t) for t in (1, 0, 2, 3)}
-
         halves = [slice(h * S // 2, (h + 1) * S // 2) for h in range(2)]
+        right_words = keep.tile([P, S], U32, name="right_words", tag="w2_low", align_bytes=64)
+        for cols in halves:
+            entries = slice(cols.start // 16, cols.stop // 16)
+            nc.vector.tensor_copy(right_words[:, cols], table_words[:].indirect(ref_list[:, entries]))
+        right = (right_words, right_scales)
+        left = (pick_words("left_words", offs_list, "w2_high"), left_scales)
+        e0 = [project("e0_%d" % h, w2_q[0], right, "e%d" % h, halves[h]) for h in range(2)]
+        e = {2: project("e2", w2_q[2], right, "e2")}
+        w1_grouped = keep.tile([P, TILES, P, PACK], BF16, name="w1_grouped", tag="w1_grouped", align_bytes=64)
+        for h in range(2):
+            nc.scalar.copy(windows[0][:, halves[h]], e0[h][:])
+        interleave_half(w1_grouped, w1_raw[0], 0)
+        nc.scalar.copy(windows[1][:, :S], project("e1", w2_q[1], right, "e0")[:])
+        interleave_half(w1_grouped, w1_raw[1], 1)
+        w1_q = quantise("w1", w1_grouped, 0, TILES)
+        y = {t: project("y%d" % t, w1_q[t], left, "y%d" % t) for t in (0, 2, 1, 3)}
+        nc.scalar.copy(windows[2][:, :S], e[2][:])
+        nc.scalar.copy(windows[3][:, :S], project("e3", w2_q[3], right, "e2")[:])
+
         last = TILES - 1
-        nc.scalar.copy(windows[1][:, :S], e[1][:])
 
         def scaled_y(name, t, scale, tag):
             tile = keep.tile([P, S], F32, name="%s%d" % (name, t), tag=tag)
             nc.scalar.activation(tile[:], y[t][:], ACT.Copy, scale=scale)
             return tile
 
-        eighth_y = {}
+        eighth_y = {t: scaled_y("eighth_y", t, 0.125, "second" if t == last else "eighth_y%d" % t) for t in range(PLAIN, TILES)}
+        g1 = [keep.tile([P, S], F32, name="first%d" % t) for t in range(PLAIN)]
+        d31 = []
+        for t in range(PLAIN):
+            d31.append(keep.tile([P, S], F32, name="third%d" % t, tag="w1_grouped" if t == PLAIN - 1 else "third%d" % t, align_bytes=64))
+            nc.vector.tensor_copy(g1[t][:], windows[t][:].indirect(c1_list[:]))
+            nc.vector.tensor_tensor(d31[t][:], windows[t][:].indirect(c3_list[:]), g1[t][:], ALU.subtract)
         minus_y = {}
-        for t in range(1, last):
-            eighth_y[t] = scaled_y("eighth_y", t, 0.125, "eighth_y%d" % t)
-            minus_y[t] = scaled_y("minus_y", t, -0.25, "minus_y%d" % t)
-            e[t + 1] = project("e%d" % (t + 1), w2_q[t + 1], right, "y%d" % t)
-        lead_banks = ["e0", "e1", "y1", "y2"]
-        outer_banks = ["outer0", "outer1", "y0", "y3"]
-        lead_turned = []
+        lead_turned = {}
         half_gap = []
         slope = {}
-        small = keep.tile([P, TILES, S], F32, name="small")
+        small = keep.tile([P, TILES, S], F32, name="small", tag="small")
         for t in range(TILES):
             half_gap.append(keep.tile([P, S], F32, name="half_gap%d" % t))
-            if t == 0:
-                g1 = keep.tile([P, S], F32, name="first0")
-                d31 = keep.tile([P, S], F32, name="third0", tag="w1_grouped", align_bytes=64)
-                nc.vector.tensor_copy(g1[:], windows[t][:].indirect(c1_list[:]))
-                nc.vector.tensor_tensor(d31[:], windows[t][:].indirect(c3_list[:]), g1[:], ALU.subtract)
-                nc.vector.scalar_tensor_tensor(half_gap[t][:], d31[:], 0.125, y[t][:], ALU.mult, ALU.mult)
+            if t < PLAIN:
+                nc.vector.scalar_tensor_tensor(half_gap[t][:], d31[t][:], 0.125, y[t][:], ALU.mult, ALU.mult)
                 terms = [half_gap[t]]
             else:
                 s1 = keep.tile([P, S], F32, name="first%d" % t)
                 s3 = keep.tile([P, S], F32, name="third%d" % t)
-                nc.vector.tensor_tensor(s1[:], windows[t][:].indirect(c1_list[:]), eighth_y[t][:], ALU.mult)
-                nc.vector.tensor_tensor(s3[:], windows[t][:].indirect(c3_list[:]), eighth_y[t][:], ALU.mult)
                 for cols in [slice(0, S)] if t < last else halves:
+                    entries = slice(cols.start // 16, cols.stop // 16)
+                    nc.vector.tensor_tensor(
+                        s1[:, cols], windows[t][:].indirect(c1_list[:, entries]), eighth_y[t][:, cols], ALU.mult
+                    )
+                    nc.vector.tensor_tensor(
+                        s3[:, cols], windows[t][:].indirect(c3_list[:, entries]), eighth_y[t][:, cols], ALU.mult
+                    )
                     nc.vector.tensor_tensor(half_gap[t][:, cols], s3[:, cols], s1[:, cols], ALU.subtract)
                 terms = [s1, s3]
-            if t + 2 < TILES:
-                nc.scalar.copy(windows[t + 2][:, :S], e[t + 2][:])
-            if t == 1:
-                eighth_y[last] = scaled_y("eighth_y", last, 0.125, "second")
-            if t == 2:
-                minus_y[last] = scaled_y("minus_y", last, -0.25, "minus_y3")
             size = keep.tile([P, S], F32, name="size%d" % t)
             for cols in [slice(0, S)] if t < last else halves:
                 nc.scalar.activation(size[:, cols], half_gap[t][:, cols], ACT.Abs)
                 nc.scalar.activation(small[:, t, cols], size[:, cols], ACT.Exp, scale=-2.0)
-            if t < last:
-                slope[t] = keep.tile([P, S], F32, name="slope%d" % t)
-                nc.scalar.activation(slope[t][:], half_gap[t][:], ACT.Tanh)
-            lead_turned.append(psum.tile([P, S], F32, name="lead_turned%d" % t, tag=lead_banks[t]))
-            turn(lead_turned[t], terms + [size], True, False)
+                if cols.start == 0:
+                    slope[t] = keep.tile([P, cols.stop], F32, name="slope%d" % t)
+                    nc.scalar.activation(slope[t][:], half_gap[t][:, cols], ACT.Tanh)
+            if t == PLAIN - 1:
+                for u in range(PLAIN, TILES):
+                    minus_y[u] = scaled_y("minus_y", u, -0.25, "minus_y%d" % u)
+            if t > 0:
+                lead_turned[t] = psum.tile([P, S], F32, name="lead_turned%d" % t, tag="e%d" % t)
+                turn(lead_turned[t], terms + [size], True, False)
 
-        second = keep.tile([P, TILES, S], F32, name="second", tag="second")
-        d21 = keep.tile([P, S], F32, name="d21")
-        nc.vector.tensor_tensor(second[:, 0, :], windows[0][:].indirect(c2_list[:]), g1[:], ALU.subtract)
-        for t in range(1, TILES):
+        second = keep.tile([P, last, S], F32, name="second", tag="second")
+        for t in range(PLAIN):
+            nc.vector.tensor_tensor(second[:, t, :], windows[t][:].indirect(c2_list[:]), g1[t][:], ALU.subtract)
+        for t in range(PLAIN):
+            s12 = keep.tile([P, S], F32, name="s12_%d" % t)
+            if t == 0:
+                nc.vector.scalar_tensor_tensor(s12[:], second[:, t, :], -0.125, y[t][:], ALU.mult, ALU.mult)
+                half_lead = keep.tile([P, S], F32, name="half_lead")
+                nc.vector.scalar_tensor_tensor(half_lead[:], half_gap[0][:], 0.0, s12[:], ALU.max, ALU.add)
+            else:
+                nc.vector.scalar_tensor_tensor(s12[:], second[:, t, :], -0.25, y[t][:], ALU.mult, ALU.mult)
+                turn(lead_turned[t], [s12], False, False)
+        for t in range(PLAIN, last):
             nc.vector.tensor_tensor(second[:, t, :], windows[t][:].indirect(c2_list[:]), minus_y[t][:], ALU.mult)
-            if t == 1:
-                nc.vector.scalar_tensor_tensor(d21[:], second[:, 0, :], -0.25, y[0][:], ALU.mult, ALU.mult)
-                turn(lead_turned[0], [d21], False, False)
             turn(lead_turned[t], [second[:, t, :]], False, False)
 
         soft = keep.tile([P, TILES, S], F32, name="soft")
         nc.scalar.activation(
             soft[:].rearrange("p t j -> p (t j)"), small[:].rearrange("p t j -> p (t j)"), ACT.Ln, bias=1.0
         )
-        for t in range(TILES):
-            turn(lead_turned[t], [soft[:, t, :]], False, True)
+        half_whole = keep.tile([P, S], F32, name="half_whole")
+        nc.vector.scalar_tensor_tensor(half_whole[:], soft[:, 0, :], 0.5, half_lead[:], ALU.mult, ALU.add)
+        for t in range(1, TILES):
+            turn(lead_turned[t], [soft[:, t, :]], False, t < last)
+        last_second = keep.tile([P, S], F32, name="last_second", tag="small")
+        nc.vector.tensor_tensor(last_second[:], windows[last][:].indirect(c2_list[:]), minus_y[last][:], ALU.mult)
+        turn(lead_turned[last], [last_second], False, True)
 
         rows = out.rearrange("(p t) j -> p t j", t=TILES)
-        outer = []
-        for t in range(TILES):
-            outer_turned = keep.tile([P, S], F32, name="outer_turned%d" % t, tag="outer_turned%d" % t)
-            nc.scalar.activation(outer_turned[:], lead_turned[t][:], ACT.Tanh, scale=0.5)
-            outer.append(psum.tile([P, S], F32, name="outer%d" % t, tag=outer_banks[t]))
-            turn(outer[t], [outer_turned], True, True)
-        slope[last] = keep.tile([P, S], F32, name="slope%d" % last, tag="outer_turned1")
-        nc.scalar.activation(slope[last][:], half_gap[last][:], ACT.Tanh)
-        for t in range(TILES):
-            for n, cols in enumerate([slice(0, S)] if t < last else halves):
-                width = cols.stop - cols.start
-                shift = keep.tile([P, width], F32, name="shift%d_%d" % (t, n))
-                nc.vector.scalar_tensor_tensor(shift[:], outer[t][:, cols], 1.0, slope[t][:, cols], ALU.add, ALU.mult)
-                result = keep.tile([P, width], F32, name="result%d_%d" % (t, n))
-                if t >= ADDS_ON_VECTOR and n == 0:
-                    nc.scalar.activation(result[:], shift[:], ACT.Identity, bias=1.0, scale=0.5)
-                    nc.scalar.dma_start(rows[:, t, cols], result[:])
-                else:
-                    nc.vector.tensor_scalar(result[:], shift[:], 0.5, 1.0, ALU.mult, ALU.add)
-                    nc.sync.dma_start(rows[:, t, cols], result[:])
+        pieces = [(t, slice(0, S)) for t in range(last)] + [(last, cols) for cols in halves]
+        outer = [keep.tile([P, S], F32, name="outer0")]
+        nc.scalar.activation(outer[0][:], half_whole[:], ACT.Tanh)
+        for n, (t, cols) in list(enumerate(pieces))[1:]:
+            width = cols.stop - cols.start
+            outer_turned = keep.tile([P, width], F32, name="outer_turned%d" % n, tag="outer_turned%d" % n)
+            nc.scalar.activation(outer_turned[:], lead_turned[t][:, cols], ACT.Tanh, scale=0.5)
+            outer.append(psum.tile([P, width], F32, name="outer%d" % n, tag="y%d" % ((n + PLAIN) % TILES)))
+            turn(outer[n], [outer_turned], True, True, width)
+        last_slope = keep.tile([P, S // 2], F32, name="last_slope", tag="outer_turned1")
+        nc.scalar.activation(last_slope[:], half_gap[last][:, halves[1]], ACT.Tanh)
+        slopes = [slope[t][:, cols] for t, cols in pieces[:-1]] + [last_slope[:]]
+        for n, (t, cols) in enumerate(pieces):
+            width = cols.stop - cols.start
+            shift = keep.tile([P, width], F32, name="shift%d" % n)
+            nc.vector.scalar_tensor_tensor(shift[:], outer[n][:], 1.0, slopes[n], ALU.add, ALU.mult)
+            result = keep.tile([P, width], F32, name="result%d" % n)
+            if n in (1, 2):
+                nc.scalar.activation(result[:], shift[:], ACT.Identity, bias=1.0, scale=0.5)
+            else:
+                nc.vector.tensor_scalar(result[:], shift[:], 0.5, 1.0, ALU.mult, ALU.add)
+            nc.sync.dma_start(rows[:, t, cols], result[:])

@@ -89,15 +89,15 @@ def tile_picked_softarg_none_p_kernel(
         def interleave_pair(name, whole, pair, copy):
             grouped = keep.tile([P, 2, P, PACK], BF16, name=name, tag=name, align_bytes=64)
             copy(
-                grouped[:].rearrange("p t m j -> p m t j"),
-                whole[:].rearrange("p j (m t) -> p m t j", t=TILES)[:, :, 2 * pair : 2 * pair + 2, :],
+                grouped[:].rearrange("p t m j -> p m j t"),
+                whole[:].rearrange("p j (m t) -> p m j t", t=TILES)[:, :, :, 2 * pair : 2 * pair + 2],
             )
             return grouped
 
         def interleave_half(grouped, raw, h):
             nc.scalar.copy(
-                grouped[:, :, h * P // 2 : (h + 1) * P // 2, :].rearrange("p t m j -> p m t j"),
-                raw.rearrange("p j (m t) -> p m t j", t=TILES),
+                grouped[:, :, h * P // 2 : (h + 1) * P // 2, :].rearrange("p t m j -> p m j t"),
+                raw.rearrange("p j (m t) -> p m j t", t=TILES),
             )
 
         def quantise(name, grouped, first, count):
@@ -246,7 +246,7 @@ def tile_picked_softarg_none_p_kernel(
             shift = keep.tile([P, width], F32, name="shift%d" % n)
             nc.vector.scalar_tensor_tensor(shift[:], outer[n][:], 1.0, slopes[n], ALU.add, ALU.mult)
             result = keep.tile([P, width], F32, name="result%d" % n)
-            if n in (1, 2):
+            if n in (1, 3):
                 nc.scalar.activation(result[:], shift[:], ACT.Identity, bias=1.0, scale=0.5)
             else:
                 nc.vector.tensor_scalar(result[:], shift[:], 0.5, 1.0, ALU.mult, ALU.add)

@@ -1,3 +1,4 @@
+import math
 from contextlib import ExitStack
 
 import concourse.mybir as mybir
@@ -167,7 +168,19 @@ def tile_picked_softarg_none_p_kernel(
         lead_turned = {}
         half_gap = []
         slope = {}
-        small = keep.tile([P, TILES, S], F32, name="small", tag="small")
+        small = keep.tile([P, 2, 2 * S], F32, name="small", tag="small")
+
+        def place(rows_tile, t, cols):
+            if t == 0:
+                return rows_tile[:, :, S + 2 * P :]
+            if t < last:
+                return rows_tile[:, t - 1, :S]
+            first = S + cols.start // 2
+            return rows_tile[:, :, first : first + P]
+
+        def in_two(ap, t):
+            return ap if 0 < t < last else ap.rearrange("p (r c) -> p r c", r=2)
+
         for t in range(TILES):
             half_gap.append(keep.tile([P, S], F32, name="half_gap%d" % t))
             if t < PLAIN:
@@ -186,19 +199,28 @@ def tile_picked_softarg_none_p_kernel(
                     )
                     nc.vector.tensor_tensor(half_gap[t][:, cols], s3[:, cols], s1[:, cols], ALU.subtract)
                 terms = [s1, s3]
+            if t == 0:
+                slope[t] = keep.tile([P, S], F32, name="slope%d" % t)
+                nc.scalar.activation(slope[t][:], half_gap[t][:], ACT.Tanh)
+                nc.scalar.activation(place(small, t, None), in_two(slope[t][:], t), ACT.Abs)
+                continue
             size = keep.tile([P, S], F32, name="size%d" % t)
             for cols in [slice(0, S)] if t < last else halves:
                 nc.scalar.activation(size[:, cols], half_gap[t][:, cols], ACT.Abs)
-                nc.scalar.activation(small[:, t, cols], size[:, cols], ACT.Exp, scale=-2.0)
+                nc.scalar.activation(place(small, t, cols), in_two(size[:, cols], t), ACT.Exp, scale=-2.0)
                 if cols.start == 0:
                     slope[t] = keep.tile([P, cols.stop], F32, name="slope%d" % t)
                     nc.scalar.activation(slope[t][:], half_gap[t][:, cols], ACT.Tanh)
             if t == PLAIN - 1:
                 for u in range(PLAIN, TILES):
                     minus_y[u] = scaled_y("minus_y", u, -0.25, "minus_y%d" % u)
-            if t > 0:
+            if t < last:
                 lead_turned[t] = psum.tile([P, S], F32, name="lead_turned%d" % t, tag="e%d" % t)
                 turn(lead_turned[t], terms + [size], True, False)
+            else:
+                for h, cols in enumerate(halves):
+                    lead_turned[t + h] = psum.tile([P, S // 2], F32, name="lead_turned%d" % (t + h), tag="e%d" % ((t + h) % TILES))
+                    turn(lead_turned[t + h], [term[:, cols] for term in terms + [size]], True, False, S // 2)
 
         second = keep.tile([P, last, S], F32, name="second", tag="second")
         for t in range(PLAIN):
@@ -216,26 +238,38 @@ def tile_picked_softarg_none_p_kernel(
             nc.vector.tensor_tensor(second[:, t, :], windows[t][:].indirect(c2_list[:]), minus_y[t][:], ALU.mult)
             turn(lead_turned[t], [second[:, t, :]], False, False)
 
-        soft = keep.tile([P, TILES, S], F32, name="soft")
-        nc.scalar.activation(
-            soft[:].rearrange("p t j -> p (t j)"), small[:].rearrange("p t j -> p (t j)"), ACT.Ln, bias=1.0
-        )
+        soft = keep.tile([P, 2, 2 * S], F32, name="soft")
+        for r in range(2):
+            nc.scalar.activation(soft[:, r, :], small[:, r, :], ACT.Ln, bias=1.0)
         half_whole = keep.tile([P, S], F32, name="half_whole")
-        nc.vector.scalar_tensor_tensor(half_whole[:], soft[:, 0, :], 0.5, half_lead[:], ALU.mult, ALU.add)
-        for t in range(1, TILES):
-            turn(lead_turned[t], [soft[:, t, :]], False, t < last)
+        nc.vector.scalar_tensor_tensor(
+            in_two(half_whole[:], 0), place(soft, 0, None), -0.5, in_two(half_lead[:], 0), ALU.mult, ALU.add
+        )
+        turn(lead_turned[1], [soft[:, 0, :S]], False, True)
+        for r in range(2):
+            if r == 1:
+                turn(lead_turned[2], [soft[:, 1, :S]], False, True)
+            for h in range(2):
+                turn(
+                    lead_turned[last + h][:, r * P : (r + 1) * P],
+                    [soft[:, r, S + h * P : S + (h + 1) * P]], False, False, P,
+                )
         last_second = keep.tile([P, S], F32, name="last_second", tag="small")
-        nc.vector.tensor_tensor(last_second[:], windows[last][:].indirect(c2_list[:]), minus_y[last][:], ALU.mult)
-        turn(lead_turned[last], [last_second], False, True)
+        for h, cols in enumerate(halves):
+            entries = slice(cols.start // 16, cols.stop // 16)
+            nc.vector.tensor_tensor(
+                last_second[:, cols], windows[last][:].indirect(c2_list[:, entries]), minus_y[last][:, cols], ALU.mult
+            )
+            turn(lead_turned[last + h], [last_second[:, cols]], False, True, S // 2)
 
         rows = out.rearrange("(p t) j -> p t j", t=TILES)
         pieces = [(t, slice(0, S)) for t in range(last)] + [(last, cols) for cols in halves]
         outer = [keep.tile([P, S], F32, name="outer0")]
-        nc.scalar.activation(outer[0][:], half_whole[:], ACT.Tanh)
+        nc.scalar.activation(outer[0][:], half_whole[:], ACT.Tanh, bias=0.5 * math.log(2.0))
         for n, (t, cols) in list(enumerate(pieces))[1:]:
             width = cols.stop - cols.start
             outer_turned = keep.tile([P, width], F32, name="outer_turned%d" % n, tag="outer_turned%d" % n)
-            nc.scalar.activation(outer_turned[:], lead_turned[t][:, cols], ACT.Tanh, scale=0.5)
+            nc.scalar.activation(outer_turned[:], lead_turned[n][:], ACT.Tanh, scale=0.5)
             outer.append(psum.tile([P, width], F32, name="outer%d" % n, tag="y%d" % ((n + PLAIN) % TILES)))
             turn(outer[n], [outer_turned], True, True, width)
         last_slope = keep.tile([P, S // 2], F32, name="last_slope", tag="outer_turned1")

@@ -21,7 +21,7 @@ P = 128
 PACK = 4
 TILES = N // P
 WINDOW = 2 * S
-PLAIN = 2
+HALF = S // 2
 
 
 def tile_picked_softarg_none_p_kernel(
@@ -38,54 +38,22 @@ def tile_picked_softarg_none_p_kernel(
             nc.sync.dma_start(tile[:], dram)
             return tile
 
-        table_scales = keep.tile([P, T], U8, name="table_scales")
-        nc.gpsimd.memset(table_scales[:].bitcast(I32), 0)
-        ref_list = load_list("ref_list", ref)
-        for q in range(4):
-            (nc.sync if q < 2 else nc.scalar).dma_start(
-                table_scales[32 * q : 32 * q + 4, :].bitcast(I32),
-                x_scales[0, 4 * q : 4 * q + 4, :].bitcast(I32),
-            )
-        offs_list = load_list("offs_list", offs)
-        w2_whole = keep.tile([P, PACK, N], F32, name="w2_whole")
-        nc.sync.dma_start(w2_whole[:], w2.rearrange("(p j) c -> p j c", j=PACK))
-        table_words = keep.tile([P, T], U32, name="table_words")
-        nc.sync.dma_start(
-            table_words[:].bitcast(I32), x_words[0].rearrange("p n t -> p (n t)").bitcast(I32)
-        )
-        c1_list = load_list("c1_list", c1)
-        c3_list = load_list("c3_list", c3)
-        windows = [keep.tile([P, WINDOW], F32, name="window%d" % t) for t in range(TILES)]
-        w1_rows = w1.rearrange("(p j) c -> p j c", j=PACK)
-        w1_raw = [windows[1 + h][:].rearrange("p (j c) -> p j c", j=PACK) for h in range(2)]
-        for h in range(2):
-            nc.sync.dma_start(w1_raw[h], w1_rows[:, :, h * N // 2 : (h + 1) * N // 2])
-        c2_list = load_list("c2_list", c2)
+        def sb(name, width=S, tag=None):
+            return keep.tile([P, width], F32, name=name, tag=tag or name, align_bytes=64)
 
-        for t in (0, 3):
-            nc.vector.memset(windows[t][:, S:], 0.0)
-
-        identity = keep.tile([P, P], F32, name="identity")
-        make_identity(nc, identity[:])
-
-        def turn(bank, terms, opens, closes, width=S):
-            count = len(terms) * (width // P)
-            for n, (term, b) in enumerate((term, b) for term in terms for b in range(width // P)):
+        def turn(bank, term, opens=False, closes=False):
+            count = term.shape[1] // P
+            for b in range(count):
                 cols = slice(b * P, (b + 1) * P)
                 nc.tensor.matmul(
                     bank[:, cols], term[:, cols], identity[:],
-                    start=opens and n == 0, stop=closes and n == count - 1, is_transpose=True,
+                    start=opens and b == 0, stop=closes and b == count - 1, is_transpose=True,
                 )
 
-        def pick_words(name, offsets, tag):
-            words = keep.tile([P, S], U32, name=name, tag=tag, align_bytes=64)
-            nc.vector.tensor_copy(words[:], table_words[:].indirect(offsets[:]))
-            return words
-
-        def pick_scales(name, offsets):
-            scales = keep.tile([P, S], U8, name=name, align_bytes=64)
-            nc.vector.tensor_copy(scales[:], table_scales[:].indirect(offsets[:]))
-            return scales
+        def pick(name, table, dtype, offsets, tag=None):
+            picked = keep.tile([P, S], dtype, name=name, tag=tag or name, align_bytes=64)
+            nc.vector.tensor_copy(picked[:], table[:].indirect(offsets[:]))
+            return picked
 
         def interleave_pair(name, whole, pair, copy):
             grouped = keep.tile([P, 2, P, PACK], BF16, name=name, tag=name, align_bytes=64)
@@ -95,19 +63,12 @@ def tile_picked_softarg_none_p_kernel(
             )
             return grouped
 
-        def interleave_half(grouped, raw, h):
-            nc.scalar.copy(
-                grouped[:, :, h * P // 2 : (h + 1) * P // 2, :].rearrange("p t m j -> p m j t"),
-                raw.rearrange("p j (m t) -> p m j t", t=TILES),
-            )
-
-        def quantise(name, grouped, first, count):
+        def quantise(name, grouped):
+            count = grouped.shape[1]
             words = keep.tile([P, count * P], U32, name=name + "_words", align_bytes=64)
             scales = keep.tile([P, count * P], U8, name=name + "_scales", align_bytes=64)
             nc.vector.quantize_mx(
-                out=words[:].bitcast(FP8X4),
-                scales=scales[:],
-                in_=grouped[:, first : first + count].rearrange("p t m j -> p (t m j)"),
+                out=words[:].bitcast(FP8X4), scales=scales[:], in_=grouped.rearrange("p t m j -> p (t m j)")
             )
             return [(words, scales, slice(i * P, (i + 1) * P)) for i in range(count)]
 
@@ -125,163 +86,192 @@ def tile_picked_softarg_none_p_kernel(
             )
             return acc
 
-        right_scales = pick_scales("right_scales", ref_list)
-        left_scales = pick_scales("left_scales", offs_list)
+        def entries(cols):
+            return slice(cols.start // 16, cols.stop // 16)
+
+        halves = [slice(0, HALF), slice(HALF, S)]
+        table_scales = keep.tile([P, T], U8, name="table_scales")
+        nc.gpsimd.memset(table_scales[:].bitcast(I32), 0)
+        ref_list = load_list("ref_list", ref)
+        offs_list = load_list("offs_list", offs)
+        for q in range(4):
+            (nc.sync if q < 2 else nc.scalar).dma_start(
+                table_scales[32 * q : 32 * q + 4, :].bitcast(I32),
+                x_scales[0, 4 * q : 4 * q + 4, :].bitcast(I32),
+            )
+        w2_whole = keep.tile([P, PACK, N], F32, name="w2_whole")
+        nc.sync.dma_start(w2_whole[:], w2.rearrange("(p j) c -> p j c", j=PACK))
+        table_words = keep.tile([P, T], U32, name="table_words")
+        nc.sync.dma_start(
+            table_words[:].bitcast(I32), x_words[0].rearrange("p n t -> p (n t)").bitcast(I32)
+        )
+        c1_list = load_list("c1_list", c1)
+        c3_list = load_list("c3_list", c3)
+        windows = [keep.tile([P, WINDOW], F32, name="window%d" % t) for t in range(TILES)]
+        w1_rows = w1.rearrange("(p j) c -> p j c", j=PACK)
+        w1_raw = [windows[2 + h][:].rearrange("p (j c) -> p j c", j=PACK) for h in range(2)]
+        for h in range(2):
+            nc.sync.dma_start(w1_raw[h], w1_rows[:, :, h * N // 2 : (h + 1) * N // 2])
+        c2_list = load_list("c2_list", c2)
+        for t in (0, 1):
+            nc.vector.memset(windows[t][:, S:], 0.0)
+        identity = keep.tile([P, P], F32, name="identity")
+        make_identity(nc, identity[:])
+
+        right_scales = pick("right_scales", table_scales, U8, ref_list)
+        left_scales = pick("left_scales", table_scales, U8, offs_list)
         w2_low = interleave_pair("w2_low", w2_whole, 0, nc.vector.tensor_copy)
         w2_high = interleave_pair("w2_high", w2_whole, 1, nc.scalar.copy)
-        w2_q = quantise("w2_low", w2_low, 0, 2) + quantise("w2_high", w2_high, 0, 2)
-        halves = [slice(h * S // 2, (h + 1) * S // 2) for h in range(2)]
+        w2_q = quantise("w2_low", w2_low[:]) + quantise("w2_high", w2_high[:])
         right_words = keep.tile([P, S], U32, name="right_words", tag="w2_low", align_bytes=64)
         for cols in halves:
-            entries = slice(cols.start // 16, cols.stop // 16)
-            nc.vector.tensor_copy(right_words[:, cols], table_words[:].indirect(ref_list[:, entries]))
+            nc.vector.tensor_copy(right_words[:, cols], table_words[:].indirect(ref_list[:, entries(cols)]))
         right = (right_words, right_scales)
-        left = (pick_words("left_words", offs_list, "w2_high"), left_scales)
-        e0 = [project("e0_%d" % h, w2_q[0], right, "e%d" % h, halves[h]) for h in range(2)]
-        e = {2: project("e2", w2_q[2], right, "e2")}
-        w1_grouped = keep.tile([P, TILES, P, PACK], BF16, name="w1_grouped", tag="w1_grouped", align_bytes=64)
-        for h in range(2):
-            nc.scalar.copy(windows[0][:, halves[h]], e0[h][:])
-        interleave_half(w1_grouped, w1_raw[0], 0)
-        nc.scalar.copy(windows[1][:, :S], project("e1", w2_q[1], right, "e0")[:])
-        interleave_half(w1_grouped, w1_raw[1], 1)
-        w1_q = quantise("w1", w1_grouped, 0, TILES)
-        y = {t: project("y%d" % t, w1_q[t], left, "y%d" % t) for t in (0, 2, 1, 3)}
-        nc.scalar.copy(windows[2][:, :S], e[2][:])
-        nc.scalar.copy(windows[3][:, :S], project("e3", w2_q[3], right, "e2")[:])
+        left = (pick("left_words", table_words, U32, offs_list, tag="w2_high"), left_scales)
 
         last = TILES - 1
+        order = (0, 1, 2, 3)
+        w1_grouped = keep.tile([P, TILES, P, PACK], BF16, name="w1_grouped", tag="w1_grouped", align_bytes=64)
 
-        def scaled_y(name, t, scale, tag):
-            tile = keep.tile([P, S], F32, name="%s%d" % (name, t), tag=tag)
+        def round_w1(h):
+            nc.scalar.copy(
+                w1_grouped[:, :, h * P // 2 : (h + 1) * P // 2, :].rearrange("p t m j -> p m j t"),
+                w1_raw[h].rearrange("p j (m t) -> p m j t", t=TILES),
+            )
+
+        def fill(t, bank):
+            nc.scalar.copy(windows[t][:, :S], project("e%d" % t, w2_q[order[t]], right, bank)[:])
+
+        def gather(dest, t, offsets, other, op, cols=slice(0, S)):
+            nc.vector.tensor_tensor(dest, windows[t][:].indirect(offsets[:, entries(cols)]), other[:, cols], op)
+
+        first = [sb("first%d" % t) for t in range(TILES)]
+        half_gap = [sb("half_gap%d" % t) for t in range(TILES)]
+        size = [sb("size%d" % t) for t in range(TILES)]
+        small = sb("small", TILES * S)
+        small_at = [slice(2 * S, 3 * S), slice(0, S), slice(3 * S, 4 * S), slice(S + HALF, 2 * S), slice(S, S + HALF)]
+        lead = {}
+        slope = {}
+
+        def gather_first(t):
+            nc.vector.tensor_copy(first[t][:], windows[t][:].indirect(c1_list[:]))
+
+        def shape(n, t, cols, terms, bank):
+            nc.scalar.activation(size[t][:, cols], half_gap[t][:, cols], ACT.Abs)
+            slope[n] = sb("slope%d" % n, cols.stop - cols.start)
+            nc.scalar.activation(slope[n][:], half_gap[t][:, cols], ACT.Tanh)
+            nc.scalar.activation(small[:, small_at[n]], size[t][:, cols], ACT.Exp, scale=-2.0)
+            lead[n] = psum.tile([P, cols.stop - cols.start], F32, name="lead%d" % n, tag=bank)
+            for k, term in enumerate(terms + [size[t]]):
+                turn(lead[n][:], term[:, cols], opens=k == 0)
+
+        def gap(t):
+            nc.vector.scalar_tensor_tensor(half_gap[t][:], third[t][:], 0.125, y[t][:], ALU.mult, ALU.mult)
+
+        e0 = [project("e0_%d" % h, w2_q[0], right, "a%d" % h, halves[h]) for h in range(2)]
+        for h in range(2):
+            nc.scalar.copy(windows[0][:, halves[h]], e0[h][:])
+        fill(1, "a2")
+        round_w1(0)
+        round_w1(1)
+        fill(2, "a0")
+        fill(3, "a1")
+        third = [sb("third0"), None, sb("third2"), sb("third3")]
+        gather_first(0)
+        gather_first(1)
+        gather(third[0][:], 0, c3_list, first[0], ALU.subtract)
+        w1_q = quantise("w1_low", w1_grouped[:, 0:2]) + quantise("w1_high", w1_grouped[:, 2:4])
+        y = {t: project("y%d" % t, w1_q[order[t]], left, "y%d" % t) for t in order}
+        third[1] = sb("third1", tag="w1_grouped")
+        gather(third[1][:], 1, c3_list, first[1], ALU.subtract)
+
+        def scaled(name, t, scale):
+            tile = sb("%s%d" % (name, t))
             nc.scalar.activation(tile[:], y[t][:], ACT.Copy, scale=scale)
             return tile
 
-        eighth_y = {t: scaled_y("eighth_y", t, 0.125, "second" if t == last else "eighth_y%d" % t) for t in range(PLAIN, TILES)}
-        g1 = [keep.tile([P, S], F32, name="first%d" % t) for t in range(PLAIN)]
-        d31 = []
-        for t in range(PLAIN):
-            d31.append(keep.tile([P, S], F32, name="third%d" % t, tag="w1_grouped" if t == PLAIN - 1 else "third%d" % t, align_bytes=64))
-            nc.vector.tensor_copy(g1[t][:], windows[t][:].indirect(c1_list[:]))
-            nc.vector.tensor_tensor(d31[t][:], windows[t][:].indirect(c3_list[:]), g1[t][:], ALU.subtract)
-        minus_y = {}
-        lead_turned = {}
-        half_gap = []
-        slope = {}
-        small = keep.tile([P, 2, 2 * S], F32, name="small", tag="small")
+        def product_gap(n, t, cols, bank):
+            nc.vector.tensor_tensor(half_gap[t][:, cols], third[t][:, cols], first[t][:, cols], ALU.subtract)
+            shape(n, t, cols, [first[t], third[t]], bank)
 
-        def place(rows_tile, t, cols):
-            if t == 0:
-                return rows_tile[:, :, S + 2 * P :]
-            if t < last:
-                return rows_tile[:, t - 1, :S]
-            first = S + cols.start // 2
-            return rows_tile[:, :, first : first + P]
+        eighth_y = {}
+        gap(0)
+        slope[0] = sb("slope0")
+        nc.scalar.activation(slope[0][:], half_gap[0][:], ACT.Tanh)
+        nc.scalar.activation(small[:, small_at[0]], slope[0][:], ACT.Abs)
+        gather_first(2)
+        gap(1)
+        eighth_y[last] = scaled("eighth_y", last, 0.125)
+        shape(1, 1, slice(0, S), [half_gap[1]], "a2")
+        minus_y = {t: scaled("minus_y", t, -0.25) for t in (last,)}
+        gather(third[2][:], 2, c3_list, first[2], ALU.subtract)
+        gap(2)
+        shape(2, 2, slice(0, S), [half_gap[2]], "a0")
+        gather(first[last][:, halves[0]], last, c1_list, eighth_y[last], ALU.mult, halves[0])
+        gather(third[last][:, halves[0]], last, c3_list, eighth_y[last], ALU.mult, halves[0])
+        gather(first[last][:, halves[1]], last, c1_list, eighth_y[last], ALU.mult, halves[1])
+        product_gap(last, last, halves[0], "a1")
+        gather(third[last][:, halves[1]], last, c3_list, eighth_y[last], ALU.mult, halves[1])
+        product_gap(last + 1, last, halves[1], "a3")
 
-        def in_two(ap, t):
-            return ap if 0 < t < last else ap.rearrange("p (r c) -> p r c", r=2)
+        second = keep.tile([P, last, S], F32, name="second", tag="eighth_y3", align_bytes=64)
+        s12 = [sb("s12_%d" % t) for t in range(last)]
 
-        for t in range(TILES):
-            half_gap.append(keep.tile([P, S], F32, name="half_gap%d" % t))
-            if t < PLAIN:
-                nc.vector.scalar_tensor_tensor(half_gap[t][:], d31[t][:], 0.125, y[t][:], ALU.mult, ALU.mult)
-                terms = [half_gap[t]]
-            else:
-                s1 = keep.tile([P, S], F32, name="first%d" % t)
-                s3 = keep.tile([P, S], F32, name="third%d" % t)
-                for cols in [slice(0, S)] if t < last else halves:
-                    entries = slice(cols.start // 16, cols.stop // 16)
-                    nc.vector.tensor_tensor(
-                        s1[:, cols], windows[t][:].indirect(c1_list[:, entries]), eighth_y[t][:, cols], ALU.mult
-                    )
-                    nc.vector.tensor_tensor(
-                        s3[:, cols], windows[t][:].indirect(c3_list[:, entries]), eighth_y[t][:, cols], ALU.mult
-                    )
-                    nc.vector.tensor_tensor(half_gap[t][:, cols], s3[:, cols], s1[:, cols], ALU.subtract)
-                terms = [s1, s3]
-            if t == 0:
-                slope[t] = keep.tile([P, S], F32, name="slope%d" % t)
-                nc.scalar.activation(slope[t][:], half_gap[t][:], ACT.Tanh)
-                nc.scalar.activation(place(small, t, None), in_two(slope[t][:], t), ACT.Abs)
-                continue
-            size = keep.tile([P, S], F32, name="size%d" % t)
-            for cols in [slice(0, S)] if t < last else halves:
-                nc.scalar.activation(size[:, cols], half_gap[t][:, cols], ACT.Abs)
-                nc.scalar.activation(place(small, t, cols), in_two(size[:, cols], t), ACT.Exp, scale=-2.0)
-                if cols.start == 0:
-                    slope[t] = keep.tile([P, cols.stop], F32, name="slope%d" % t)
-                    nc.scalar.activation(slope[t][:], half_gap[t][:, cols], ACT.Tanh)
-            if t == PLAIN - 1:
-                for u in range(PLAIN, TILES):
-                    minus_y[u] = scaled_y("minus_y", u, -0.25, "minus_y%d" % u)
-            if t < last:
-                lead_turned[t] = psum.tile([P, S], F32, name="lead_turned%d" % t, tag="e%d" % t)
-                turn(lead_turned[t], terms + [size], True, False)
-            else:
-                for h, cols in enumerate(halves):
-                    lead_turned[t + h] = psum.tile([P, S // 2], F32, name="lead_turned%d" % (t + h), tag="e%d" % ((t + h) % TILES))
-                    turn(lead_turned[t + h], [term[:, cols] for term in terms + [size]], True, False, S // 2)
+        def score(t, scale):
+            nc.vector.scalar_tensor_tensor(s12[t][:], second[:, t, :], scale, y[t][:], ALU.mult, ALU.mult)
 
-        second = keep.tile([P, last, S], F32, name="second", tag="second")
-        for t in range(PLAIN):
-            nc.vector.tensor_tensor(second[:, t, :], windows[t][:].indirect(c2_list[:]), g1[t][:], ALU.subtract)
-        for t in range(PLAIN):
-            s12 = keep.tile([P, S], F32, name="s12_%d" % t)
-            if t == 0:
-                nc.vector.scalar_tensor_tensor(s12[:], second[:, t, :], -0.125, y[t][:], ALU.mult, ALU.mult)
-                half_lead = keep.tile([P, S], F32, name="half_lead")
-                nc.vector.scalar_tensor_tensor(half_lead[:], half_gap[0][:], 0.0, s12[:], ALU.max, ALU.add)
-            else:
-                nc.vector.scalar_tensor_tensor(s12[:], second[:, t, :], -0.25, y[t][:], ALU.mult, ALU.mult)
-                turn(lead_turned[t], [s12], False, False)
-        for t in range(PLAIN, last):
-            nc.vector.tensor_tensor(second[:, t, :], windows[t][:].indirect(c2_list[:]), minus_y[t][:], ALU.mult)
-            turn(lead_turned[t], [second[:, t, :]], False, False)
-
-        soft = keep.tile([P, 2, 2 * S], F32, name="soft")
-        for r in range(2):
-            nc.scalar.activation(soft[:, r, :], small[:, r, :], ACT.Ln, bias=1.0)
-        half_whole = keep.tile([P, S], F32, name="half_whole")
-        nc.vector.scalar_tensor_tensor(
-            in_two(half_whole[:], 0), place(soft, 0, None), -0.5, in_two(half_lead[:], 0), ALU.mult, ALU.add
-        )
-        turn(lead_turned[1], [soft[:, 0, :S]], False, True)
-        for r in range(2):
-            if r == 1:
-                turn(lead_turned[2], [soft[:, 1, :S]], False, True)
-            for h in range(2):
-                turn(
-                    lead_turned[last + h][:, r * P : (r + 1) * P],
-                    [soft[:, r, S + h * P : S + (h + 1) * P]], False, False, P,
-                )
-        last_second = keep.tile([P, S], F32, name="last_second", tag="small")
+        soft = sb("soft", TILES * S)
+        cut = S + P
+        nc.scalar.activation(soft[:, :cut], small[:, :cut], ACT.Ln, bias=1.0)
+        nc.scalar.activation(soft[:, cut:], small[:, cut:], ACT.Ln, bias=1.0)
+        for t in range(2):
+            gather(second[:, t, :], t, c2_list, first[t], ALU.subtract)
+        score(0, -0.125)
+        gather(second[:, 2, :], 2, c2_list, first[2], ALU.subtract)
+        score(1, -0.25)
+        half_lead = sb("half_lead")
+        nc.vector.scalar_tensor_tensor(half_lead[:], half_gap[0][:], 0.0, s12[0][:], ALU.max, ALU.add)
+        score(2, -0.25)
+        half_whole = sb("half_whole")
+        nc.vector.scalar_tensor_tensor(half_whole[:], soft[:, small_at[0]], -0.5, half_lead[:], ALU.mult, ALU.add)
+        turn(lead[1][:], s12[1][:])
+        turn(lead[1][:], soft[:, small_at[1]], closes=True)
+        turn(lead[2][:], soft[:, small_at[2]])
+        turn(lead[2][:], s12[2][:], closes=True)
+        last_second = sb("last_second", tag="small")
         for h, cols in enumerate(halves):
-            entries = slice(cols.start // 16, cols.stop // 16)
-            nc.vector.tensor_tensor(
-                last_second[:, cols], windows[last][:].indirect(c2_list[:, entries]), minus_y[last][:, cols], ALU.mult
-            )
-            turn(lead_turned[last + h], [last_second[:, cols]], False, True, S // 2)
+            turn(lead[last + h][:], soft[:, small_at[last + h]])
+        for h, cols in enumerate(halves):
+            gather(last_second[:, cols], last, c2_list, minus_y[last], ALU.mult, cols)
+            turn(lead[last + h][:], last_second[:, cols], closes=True)
 
         rows = out.rearrange("(p t) j -> p t j", t=TILES)
         pieces = [(t, slice(0, S)) for t in range(last)] + [(last, cols) for cols in halves]
-        outer = [keep.tile([P, S], F32, name="outer0")]
-        nc.scalar.activation(outer[0][:], half_whole[:], ACT.Tanh, bias=0.5 * math.log(2.0))
-        for n, (t, cols) in list(enumerate(pieces))[1:]:
-            width = cols.stop - cols.start
-            outer_turned = keep.tile([P, width], F32, name="outer_turned%d" % n, tag="outer_turned%d" % n)
-            nc.scalar.activation(outer_turned[:], lead_turned[n][:], ACT.Tanh, scale=0.5)
-            outer.append(psum.tile([P, width], F32, name="outer%d" % n, tag="y%d" % ((n + PLAIN) % TILES)))
-            turn(outer[n], [outer_turned], True, True, width)
-        last_slope = keep.tile([P, S // 2], F32, name="last_slope", tag="outer_turned1")
-        nc.scalar.activation(last_slope[:], half_gap[last][:, halves[1]], ACT.Tanh)
-        slopes = [slope[t][:, cols] for t, cols in pieces[:-1]] + [last_slope[:]]
-        for n, (t, cols) in enumerate(pieces):
-            width = cols.stop - cols.start
-            shift = keep.tile([P, width], F32, name="shift%d" % n)
-            nc.vector.scalar_tensor_tensor(shift[:], outer[n][:], 1.0, slopes[n], ALU.add, ALU.mult)
-            result = keep.tile([P, width], F32, name="result%d" % n)
-            if n in (1, 3):
-                nc.scalar.activation(result[:], shift[:], ACT.Identity, bias=1.0, scale=0.5)
+        outer = {}
+        for n in (1, 0, 2, 3, 4):
+            width = pieces[n][1].stop - pieces[n][1].start
+            if n == 0:
+                outer[n] = sb("outer0")
+                nc.scalar.activation(outer[n][:], half_whole[:], ACT.Tanh, bias=0.5 * math.log(2.0))
             else:
-                nc.vector.tensor_scalar(result[:], shift[:], 0.5, 1.0, ALU.mult, ALU.add)
-            nc.sync.dma_start(rows[:, t, cols], result[:])
+                outer_turned = sb("outer_turned%d" % n, width)
+                nc.scalar.activation(outer_turned[:], lead[n][:], ACT.Tanh, scale=0.5)
+                outer[n] = psum.tile([P, width], F32, name="outer%d" % n, tag="y%d" % ((n + 2) % TILES))
+                turn(outer[n][:], outer_turned[:], opens=True, closes=True)
+        shifts = []
+
+        def finish(n):
+            t, cols = pieces[n]
+            result = sb("result%d" % n, cols.stop - cols.start)
+            if n in (1, 3):
+                nc.scalar.activation(result[:], shifts[n][:], ACT.Identity, bias=1.0, scale=0.5)
+            else:
+                nc.vector.tensor_scalar(result[:], shifts[n][:], 0.5, 1.0, ALU.mult, ALU.add)
+            nc.sync.dma_start(rows[:, order[t], cols], result[:])
+
+        for n, (t, cols) in enumerate(pieces):
+            shifts.append(sb("shift%d" % n, cols.stop - cols.start))
+            nc.vector.scalar_tensor_tensor(shifts[n][:], outer[n][:], 1.0, slope[n][:], ALU.add, ALU.mult)
+            if n > 0:
+                finish(n - 1)
+        finish(len(pieces) - 1)

@@ -59,7 +59,7 @@ def tile_picked_softarg_none_p_kernel(
             grouped = keep.tile([P, 2, P, PACK], BF16, name=name, tag=name, align_bytes=64)
             copy(
                 grouped[:].rearrange("p t m j -> p m j t"),
-                whole[:].rearrange("p j (m t) -> p m j t", t=TILES)[:, :, :, 2 * pair : 2 * pair + 2],
+                whole.rearrange("p j (m t) -> p m j t", t=TILES)[:, :, :, 2 * pair : 2 * pair + 2],
             )
             return grouped
 
@@ -99,22 +99,19 @@ def tile_picked_softarg_none_p_kernel(
                 table_scales[32 * q : 32 * q + 4, :].bitcast(I32),
                 x_scales[0, 4 * q : 4 * q + 4, :].bitcast(I32),
             )
-        w2_whole = keep.tile([P, PACK, N], F32, name="w2_whole")
-        nc.sync.dma_start(w2_whole[:], w2.rearrange("(p j) c -> p j c", j=PACK))
+        shared = ctx.enter_context(tc.tile_pool(name="shared", bufs=1))
+        w2_whole = shared.tile([P, PACK, N], F32, name="w2_whole", offset=0)[:]
+        w1_whole = shared.tile([P, PACK, N], F32, name="w1_whole", offset=2 * WINDOW * 4)[:]
+        windows = [shared.tile([P, WINDOW], F32, name="window%d" % t, offset=(0, 2, 3, 1)[t] * WINDOW * 4) for t in range(TILES)]
+        nc.sync.dma_start(w2_whole, w2.rearrange("(p j) c -> p j c", j=PACK))
         table_words = keep.tile([P, T], U32, name="table_words")
         nc.sync.dma_start(
             table_words[:].bitcast(I32), x_words[0].rearrange("p n t -> p (n t)").bitcast(I32)
         )
         c1_list = load_list("c1_list", c1)
         c3_list = load_list("c3_list", c3)
-        windows = [keep.tile([P, WINDOW], F32, name="window%d" % t) for t in range(TILES)]
-        w1_rows = w1.rearrange("(p j) c -> p j c", j=PACK)
-        w1_raw = [windows[2 + h][:].rearrange("p (j c) -> p j c", j=PACK) for h in range(2)]
-        for h in range(2):
-            nc.sync.dma_start(w1_raw[h], w1_rows[:, :, h * N // 2 : (h + 1) * N // 2])
+        nc.sync.dma_start(w1_whole, w1.rearrange("(p j) c -> p j c", j=PACK))
         c2_list = load_list("c2_list", c2)
-        for t in (0, 1):
-            nc.vector.memset(windows[t][:, S:], 0.0)
         identity = keep.tile([P, P], F32, name="identity")
         make_identity(nc, identity[:])
 
@@ -130,148 +127,138 @@ def tile_picked_softarg_none_p_kernel(
         left = (pick("left_words", table_words, U32, offs_list, tag="w2_high"), left_scales)
 
         last = TILES - 1
-        order = (0, 1, 2, 3)
-        w1_grouped = keep.tile([P, TILES, P, PACK], BF16, name="w1_grouped", tag="w1_grouped", align_bytes=64)
+        w1_grouped = keep.tile([P, TILES, P, PACK], BF16, name="w1_grouped", align_bytes=64)
 
         def round_w1(h):
             nc.scalar.copy(
                 w1_grouped[:, :, h * P // 2 : (h + 1) * P // 2, :].rearrange("p t m j -> p m j t"),
-                w1_raw[h].rearrange("p j (m t) -> p m j t", t=TILES),
+                w1_whole[:, :, h * N // 2 : (h + 1) * N // 2].rearrange("p j (m t) -> p m j t", t=TILES),
             )
 
         def fill(t, bank):
-            nc.scalar.copy(windows[t][:, :S], project("e%d" % t, w2_q[order[t]], right, bank)[:])
+            nc.scalar.copy(windows[t][:, :S], project("e%d" % t, w2_q[t], right, bank)[:])
 
-        def gather(dest, t, offsets, other, op, cols=slice(0, S)):
-            nc.vector.tensor_tensor(dest, windows[t][:].indirect(offsets[:, entries(cols)]), other[:, cols], op)
-
-        first = [sb("first%d" % t) for t in range(TILES)]
+        first = [sb("first%d" % t) for t in range(last)]
+        third = [sb("third%d" % t) for t in range(last)]
         half_gap = [sb("half_gap%d" % t) for t in range(TILES)]
         size = [sb("size%d" % t) for t in range(TILES)]
         small = sb("small", TILES * S)
-        small_at = [slice(2 * S, 3 * S), slice(0, S), slice(3 * S, 4 * S), slice(S + HALF, 2 * S), slice(S, S + HALF)]
+        small_at = [slice(0, S), slice(2 * S, 3 * S), slice(3 * S, 4 * S), slice(S, 2 * S)]
         lead = {}
         slope = {}
 
-        def gather_first(t):
-            nc.vector.tensor_copy(first[t][:], windows[t][:].indirect(c1_list[:]))
+        def gather_first(t, parts=(slice(0, S),)):
+            for cols in parts:
+                nc.vector.tensor_copy(first[t][:, cols], windows[t][:].indirect(c1_list[:, entries(cols)]))
 
-        def shape(n, t, cols, terms, bank):
+        def gather(dest, t, offsets, cols=slice(0, S)):
+            nc.vector.tensor_tensor(dest, windows[t][:].indirect(offsets[:, entries(cols)]), first[t][:, cols], ALU.subtract)
+
+        def shape(n, t, cols, bank):
             nc.scalar.activation(size[t][:, cols], half_gap[t][:, cols], ACT.Abs)
             slope[n] = sb("slope%d" % n, cols.stop - cols.start)
             nc.scalar.activation(slope[n][:], half_gap[t][:, cols], ACT.Tanh)
             nc.scalar.activation(small[:, small_at[n]], size[t][:, cols], ACT.Exp, scale=-2.0)
             lead[n] = psum.tile([P, cols.stop - cols.start], F32, name="lead%d" % n, tag=bank)
-            for k, term in enumerate(terms + [size[t]]):
-                turn(lead[n][:], term[:, cols], opens=k == 0)
+            turn(lead[n][:], half_gap[t][:, cols], opens=True)
+            turn(lead[n][:], size[t][:, cols])
 
-        def gap(t):
-            nc.vector.scalar_tensor_tensor(half_gap[t][:], third[t][:], 0.125, y[t][:], ALU.mult, ALU.mult)
+        def times_y(dest, src, t, scale, cols=slice(0, S)):
+            nc.vector.scalar_tensor_tensor(dest[:, cols], src[:, cols], scale, y[t][:, cols], ALU.mult, ALU.mult)
 
         e0 = [project("e0_%d" % h, w2_q[0], right, "a%d" % h, halves[h]) for h in range(2)]
         for h in range(2):
             nc.scalar.copy(windows[0][:, halves[h]], e0[h][:])
-        fill(1, "a2")
         round_w1(0)
         round_w1(1)
-        fill(2, "a0")
-        fill(3, "a1")
-        third = [sb("third0"), None, sb("third2"), sb("third3")]
-        gather_first(0)
-        gather_first(1)
-        gather(third[0][:], 0, c3_list, first[0], ALU.subtract)
+        for t in range(1, TILES):
+            fill(t, "a%d" % (2 + (t + 1) % 2))
+        gather_first(0, halves)
+        for cols in halves:
+            gather(third[0][:, cols], 0, c3_list, cols)
         w1_q = quantise("w1_low", w1_grouped[:, 0:2]) + quantise("w1_high", w1_grouped[:, 2:4])
-        y = {t: project("y%d" % t, w1_q[order[t]], left, "y%d" % t) for t in order}
-        third[1] = sb("third1", tag="w1_grouped")
-        gather(third[1][:], 1, c3_list, first[1], ALU.subtract)
+        y = [project("y%d" % t, w1_q[t], left, "y%d" % t) for t in range(TILES)]
+        gather_first(1)
+        times_y(half_gap[0], third[0], 0, 0.125)
+        eighth_y = {t: sb("eighth_y%d" % t) for t in range(1, TILES)}
+        for t in (1, 2):
+            nc.scalar.activation(eighth_y[t][:], y[t][:], ACT.Copy, scale=0.125)
+        shape(0, 0, slice(0, S), "a0")
+        nc.scalar.activation(eighth_y[last][:], y[last][:], ACT.Copy, scale=0.125)
+        gather(third[1][:], 1, c3_list)
+        nc.gpsimd.tensor_tensor(half_gap[1][:], third[1][:], eighth_y[1][:], ALU.mult)
+        gather_first(2, halves)
+        shape(1, 1, slice(0, S), "a1")
+        for cols in halves:
+            gather(third[2][:, cols], 2, c3_list, cols)
+        nc.gpsimd.tensor_tensor(half_gap[2][:], third[2][:], eighth_y[2][:], ALU.mult)
+        first.append(sb("first3", tag="third1"))
+        gather_first(last, halves)
+        shape(2, 2, slice(0, S), "a3")
+        third_last = [sb("third3_0", HALF, tag="second"), sb("third3_1", HALF)]
+        for h, cols in enumerate(halves):
+            gather(third_last[h][:], last, c3_list, cols)
+        slope[last] = sb("slope3")
+        for h, cols in enumerate(halves):
+            nc.vector.scalar_tensor_tensor(half_gap[last][:, cols], third_last[h][:], 0.125, y[last][:, cols], ALU.mult, ALU.mult)
+            nc.scalar.activation(slope[last][:, cols], half_gap[last][:, cols], ACT.Tanh)
+        for cols in halves:
+            nc.scalar.activation(small[:, small_at[last]][:, cols], slope[last][:, cols], ACT.Abs)
 
-        def scaled(name, t, scale):
-            tile = sb("%s%d" % (name, t))
-            nc.scalar.activation(tile[:], y[t][:], ACT.Copy, scale=scale)
-            return tile
-
-        def product_gap(n, t, cols, bank):
-            nc.vector.tensor_tensor(half_gap[t][:, cols], third[t][:, cols], first[t][:, cols], ALU.subtract)
-            shape(n, t, cols, [first[t], third[t]], bank)
-
-        eighth_y = {}
-        gap(0)
-        slope[0] = sb("slope0")
-        nc.scalar.activation(slope[0][:], half_gap[0][:], ACT.Tanh)
-        nc.scalar.activation(small[:, small_at[0]], slope[0][:], ACT.Abs)
-        gather_first(2)
-        gap(1)
-        eighth_y[last] = scaled("eighth_y", last, 0.125)
-        shape(1, 1, slice(0, S), [half_gap[1]], "a2")
-        minus_y = {t: scaled("minus_y", t, -0.25) for t in (last,)}
-        gather(third[2][:], 2, c3_list, first[2], ALU.subtract)
-        gap(2)
-        shape(2, 2, slice(0, S), [half_gap[2]], "a0")
-        gather(first[last][:, halves[0]], last, c1_list, eighth_y[last], ALU.mult, halves[0])
-        gather(third[last][:, halves[0]], last, c3_list, eighth_y[last], ALU.mult, halves[0])
-        gather(first[last][:, halves[1]], last, c1_list, eighth_y[last], ALU.mult, halves[1])
-        product_gap(last, last, halves[0], "a1")
-        gather(third[last][:, halves[1]], last, c3_list, eighth_y[last], ALU.mult, halves[1])
-        product_gap(last + 1, last, halves[1], "a3")
-
-        second = keep.tile([P, last, S], F32, name="second", tag="eighth_y3", align_bytes=64)
-        s12 = [sb("s12_%d" % t) for t in range(last)]
-
-        def score(t, scale):
-            nc.vector.scalar_tensor_tensor(s12[t][:], second[:, t, :], scale, y[t][:], ALU.mult, ALU.mult)
-
+        second = keep.tile([P, TILES, S], F32, name="second", tag="second", align_bytes=64)
+        s12 = [sb("s12_%d" % t) for t in range(TILES)]
         soft = sb("soft", TILES * S)
-        cut = S + P
+        cut = 2 * S - P
         nc.scalar.activation(soft[:, :cut], small[:, :cut], ACT.Ln, bias=1.0)
         nc.scalar.activation(soft[:, cut:], small[:, cut:], ACT.Ln, bias=1.0)
+        for t in (0, 1, last):
+            gather(second[:, t, :], t, c2_list)
+        nc.gpsimd.tensor_tensor(s12[last][:], second[:, last, :], eighth_y[last][:], ALU.mult)
         for t in range(2):
-            gather(second[:, t, :], t, c2_list, first[t], ALU.subtract)
-        score(0, -0.125)
-        gather(second[:, 2, :], 2, c2_list, first[2], ALU.subtract)
-        score(1, -0.25)
+            times_y(s12[t], second[:, t, :], t, -0.25)
         half_lead = sb("half_lead")
-        nc.vector.scalar_tensor_tensor(half_lead[:], half_gap[0][:], 0.0, s12[0][:], ALU.max, ALU.add)
-        score(2, -0.25)
+        nc.vector.scalar_tensor_tensor(half_lead[:], half_gap[last][:], 0.0, s12[last][:], ALU.max, ALU.subtract)
+        late_second = sb("late_second", tag="small")
+        gather(late_second[:, halves[0]], 2, c2_list, halves[0])
         half_whole = sb("half_whole")
-        nc.vector.scalar_tensor_tensor(half_whole[:], soft[:, small_at[0]], -0.5, half_lead[:], ALU.mult, ALU.add)
+        nc.vector.scalar_tensor_tensor(half_whole[:], soft[:, small_at[last]], -0.5, half_lead[:], ALU.mult, ALU.add)
+        gather(late_second[:, halves[1]], 2, c2_list, halves[1])
+        for cols in halves:
+            times_y(s12[2], late_second, 2, -0.25, cols)
+        turn(lead[0][:], s12[0][:])
+        turn(lead[0][:], soft[:, small_at[0]], closes=True)
         turn(lead[1][:], s12[1][:])
         turn(lead[1][:], soft[:, small_at[1]], closes=True)
         turn(lead[2][:], soft[:, small_at[2]])
         turn(lead[2][:], s12[2][:], closes=True)
-        last_second = sb("last_second", tag="small")
-        for h, cols in enumerate(halves):
-            turn(lead[last + h][:], soft[:, small_at[last + h]])
-        for h, cols in enumerate(halves):
-            gather(last_second[:, cols], last, c2_list, minus_y[last], ALU.mult, cols)
-            turn(lead[last + h][:], last_second[:, cols], closes=True)
 
         rows = out.rearrange("(p t) j -> p t j", t=TILES)
-        pieces = [(t, slice(0, S)) for t in range(last)] + [(last, cols) for cols in halves]
-        outer = {}
-        for n in (1, 0, 2, 3, 4):
-            width = pieces[n][1].stop - pieces[n][1].start
-            if n == 0:
-                outer[n] = sb("outer0")
+        pieces = [(last, slice(0, S), None), (0, slice(0, S), "y0"), (1, slice(0, S), "y1"), (2, halves[0], "y3"), (2, halves[1], "a2")]
+        outer = []
+        for n, (t, cols, bank) in enumerate(pieces):
+            width = cols.stop - cols.start
+            if t == last:
+                outer.append(sb("outer%d" % n))
                 nc.scalar.activation(outer[n][:], half_whole[:], ACT.Tanh, bias=0.5 * math.log(2.0))
             else:
                 outer_turned = sb("outer_turned%d" % n, width)
-                nc.scalar.activation(outer_turned[:], lead[n][:], ACT.Tanh, scale=0.5)
-                outer[n] = psum.tile([P, width], F32, name="outer%d" % n, tag="y%d" % ((n + 2) % TILES))
+                nc.scalar.activation(outer_turned[:], lead[t][:, cols], ACT.Tanh, scale=0.5)
+                outer.append(psum.tile([P, width], F32, name="outer%d" % n, tag=bank))
                 turn(outer[n][:], outer_turned[:], opens=True, closes=True)
         shifts = []
 
         def finish(n):
-            t, cols = pieces[n]
+            t, cols, bank = pieces[n]
             result = sb("result%d" % n, cols.stop - cols.start)
-            if n in (1, 3):
+            if n == 2:
                 nc.scalar.activation(result[:], shifts[n][:], ACT.Identity, bias=1.0, scale=0.5)
             else:
-                nc.vector.tensor_scalar(result[:], shifts[n][:], 0.5, 1.0, ALU.mult, ALU.add)
-            nc.sync.dma_start(rows[:, order[t], cols], result[:])
+                (nc.gpsimd if n < 2 else nc.vector).tensor_scalar(result[:], shifts[n][:], 0.5, 1.0, ALU.mult, ALU.add)
+            nc.sync.dma_start(rows[:, t, cols], result[:])
 
-        for n, (t, cols) in enumerate(pieces):
+        for n, (t, cols, bank) in enumerate(pieces):
             shifts.append(sb("shift%d" % n, cols.stop - cols.start))
-            nc.vector.scalar_tensor_tensor(shifts[n][:], outer[n][:], 1.0, slope[n][:], ALU.add, ALU.mult)
+            nc.vector.scalar_tensor_tensor(shifts[n][:], outer[n][:], 1.0, slope[t][:, cols], ALU.add, ALU.mult)
             if n > 0:
                 finish(n - 1)
         finish(len(pieces) - 1)

@@ -91,7 +91,7 @@ def tile_picked_softarg_none_p_kernel(
 
         halves = [slice(0, HALF), slice(HALF, S)]
         table_scales = keep.tile([P, T], U8, name="table_scales")
-        nc.gpsimd.memset(table_scales[:].bitcast(I32), 0)
+        nc.vector.memset(table_scales[:].bitcast(I32), 0)
         ref_list = load_list("ref_list", ref)
         offs_list = load_list("offs_list", offs)
         for q in range(4):
@@ -251,9 +251,12 @@ def tile_picked_softarg_none_p_kernel(
             t, cols, bank = pieces[n]
             result = sb("result%d" % n, cols.stop - cols.start)
             if n == 2:
+                nc.scalar.activation(result[:, halves[0]], shifts[n][:, halves[0]], ACT.Identity, bias=1.0, scale=0.5)
+                nc.gpsimd.tensor_scalar(result[:, halves[1]], shifts[n][:, halves[1]], 0.5, 1.0, ALU.mult, ALU.add)
+            elif n == 1:
                 nc.scalar.activation(result[:], shifts[n][:], ACT.Identity, bias=1.0, scale=0.5)
             else:
-                (nc.gpsimd if n < 2 else nc.vector).tensor_scalar(result[:], shifts[n][:], 0.5, 1.0, ALU.mult, ALU.add)
+                (nc.gpsimd if n == 0 else nc.vector).tensor_scalar(result[:], shifts[n][:], 0.5, 1.0, ALU.mult, ALU.add)
             nc.sync.dma_start(rows[:, t, cols], result[:])
 
         for n, (t, cols, bank) in enumerate(pieces):

@@ -233,7 +233,9 @@ def tile_picked_softarg_none_p_kernel(
         turn(lead[2][:], s12[2][:], closes=True)
 
         rows = out.rearrange("(p t) j -> p t j", t=TILES)
-        pieces = [(last, slice(0, S), None), (0, slice(0, S), "y0"), (1, slice(0, S), "y1"), (2, halves[0], "y3"), (2, halves[1], "a2")]
+        pieces = [(last, slice(0, S), None)] + [
+            (n // 2, halves[n % 2], bank) for n, bank in enumerate(("y0", "y1", "y3", "a2", "a0", "y2"))
+        ]
         outer = []
         for n, (t, cols, bank) in enumerate(pieces):
             width = cols.stop - cols.start
@@ -245,23 +247,20 @@ def tile_picked_softarg_none_p_kernel(
                 nc.scalar.activation(outer_turned[:], lead[t][:, cols], ACT.Tanh, scale=0.5)
                 outer.append(psum.tile([P, width], F32, name="outer%d" % n, tag=bank))
                 turn(outer[n][:], outer_turned[:], opens=True, closes=True)
-        shifts = []
+        shift = [sb("shift%d" % t) for t in range(TILES)]
+        result = [sb("result%d" % t) for t in range(TILES)]
 
-        def finish(n):
-            t, cols, bank = pieces[n]
-            result = sb("result%d" % n, cols.stop - cols.start)
-            if n == 2:
-                nc.scalar.activation(result[:, halves[0]], shifts[n][:, halves[0]], ACT.Identity, bias=1.0, scale=0.5)
-                nc.gpsimd.tensor_scalar(result[:, halves[1]], shifts[n][:, halves[1]], 0.5, 1.0, ALU.mult, ALU.add)
-            elif n == 1:
-                nc.scalar.activation(result[:], shifts[n][:], ACT.Identity, bias=1.0, scale=0.5)
-            else:
-                (nc.gpsimd if n == 0 else nc.vector).tensor_scalar(result[:], shifts[n][:], 0.5, 1.0, ALU.mult, ALU.add)
-            nc.sync.dma_start(rows[:, t, cols], result[:])
+        def finish(engine, t, cols):
+            engine.tensor_scalar(result[t][:, cols], shift[t][:, cols], 0.5, 1.0, ALU.mult, ALU.add)
 
         for n, (t, cols, bank) in enumerate(pieces):
-            shifts.append(sb("shift%d" % n, cols.stop - cols.start))
-            nc.vector.scalar_tensor_tensor(shifts[n][:], outer[n][:], 1.0, slope[t][:, cols], ALU.add, ALU.mult)
-            if n > 0:
-                finish(n - 1)
-        finish(len(pieces) - 1)
+            nc.vector.scalar_tensor_tensor(shift[t][:, cols], outer[n][:], 1.0, slope[t][:, cols], ALU.add, ALU.mult)
+        finish(nc.gpsimd, last, slice(0, S))
+        nc.sync.dma_start(rows[:, last, :], result[last][:])
+        for t in range(2):
+            finish(nc.gpsimd, t, halves[0])
+            nc.scalar.activation(result[t][:, halves[1]], shift[t][:, halves[1]], ACT.Identity, bias=1.0, scale=0.5)
+            nc.sync.dma_start(rows[:, t, :], result[t][:])
+        for cols in halves:
+            finish(nc.vector, 2, cols)
+            nc.sync.dma_start(rows[:, 2, cols], result[2][:, cols])

@@ -20,8 +20,8 @@ ACT = mybir.ActivationFunctionType
 P = 128
 PACK = 4
 TILES = N // P
-WINDOW = 2 * S
 HALF = S // 2
+WINDOW = 2 * S
 
 
 def tile_picked_softarg_none_p_kernel(
@@ -95,7 +95,7 @@ def tile_picked_softarg_none_p_kernel(
         ref_list = load_list("ref_list", ref)
         offs_list = load_list("offs_list", offs)
         for q in range(4):
-            (nc.sync if q < 2 else nc.scalar).dma_start(
+            nc.sync.dma_start(
                 table_scales[32 * q : 32 * q + 4, :].bitcast(I32),
                 x_scales[0, 4 * q : 4 * q + 4, :].bitcast(I32),
             )
@@ -138,8 +138,8 @@ def tile_picked_softarg_none_p_kernel(
         def fill(t, bank):
             nc.scalar.copy(windows[t][:, :S], project("e%d" % t, w2_q[t], right, bank)[:])
 
-        first = [sb("first%d" % t) for t in range(last)]
-        third = [sb("third%d" % t) for t in range(last)]
+        first = {t: sb("first%d" % t) for t in range(last)}
+        third = {t: sb("third%d" % t) for t in range(last)}
         half_gap = [sb("half_gap%d" % t) for t in range(TILES)]
         size = [sb("size%d" % t) for t in range(TILES)]
         small = sb("small", TILES * S)
@@ -184,25 +184,35 @@ def tile_picked_softarg_none_p_kernel(
         for t in (1, 2):
             nc.scalar.activation(eighth_y[t][:], y[t][:], ACT.Copy, scale=0.125)
         shape(0, 0, slice(0, S), "a0")
-        nc.scalar.activation(eighth_y[last][:], y[last][:], ACT.Copy, scale=0.125)
+        nc.scalar.activation(eighth_y[last][:], y[last][:], ACT.Copy, scale=0.25)
         gather(third[1][:], 1, c3_list)
         nc.gpsimd.tensor_tensor(half_gap[1][:], third[1][:], eighth_y[1][:], ALU.mult)
         gather_first(2, halves)
         shape(1, 1, slice(0, S), "a1")
         for cols in halves:
             gather(third[2][:, cols], 2, c3_list, cols)
-        nc.gpsimd.tensor_tensor(half_gap[2][:], third[2][:], eighth_y[2][:], ALU.mult)
-        first.append(sb("first3", tag="third1"))
+        first[last] = sb("first3", tag="third1")
         gather_first(last, halves)
-        shape(2, 2, slice(0, S), "a3")
-        third_last = [sb("third3_0", HALF, tag="second"), sb("third3_1", HALF)]
+        slope[2] = sb("slope2")
+        lead[2] = psum.tile([P, S], F32, name="lead2", tag="a3")
+        for n, blocks in enumerate((slice(1, 3), slice(0, 4, 3))):
+            def part(tile, blocks=blocks):
+                return tile.rearrange("p (b c) -> p b c", c=P)[:, blocks, :]
+            nc.gpsimd.tensor_tensor(part(half_gap[2][:]), part(third[2][:]), part(eighth_y[2][:]), ALU.mult)
+            nc.scalar.activation(part(size[2][:]), part(half_gap[2][:]), ACT.Abs)
+            nc.scalar.activation(part(small[:, small_at[2]]), part(size[2][:]), ACT.Exp, scale=-2.0)
+            nc.scalar.activation(part(slope[2][:]), part(half_gap[2][:]), ACT.Tanh)
+            for term in (half_gap[2], size[2]):
+                for k in range(4)[blocks]:
+                    cols = slice(k * P, (k + 1) * P)
+                    turn(lead[2][:, cols], term[:, cols], opens=n == 0 and k == 1 and term is half_gap[2])
+        third_last = [sb("third3_0", HALF, tag="second"), sb("third3_1", HALF, tag="third3_1")]
         for h, cols in enumerate(halves):
             gather(third_last[h][:], last, c3_list, cols)
         slope[last] = sb("slope3")
         for h, cols in enumerate(halves):
-            nc.vector.scalar_tensor_tensor(half_gap[last][:, cols], third_last[h][:], 0.125, y[last][:, cols], ALU.mult, ALU.mult)
-            nc.scalar.activation(slope[last][:, cols], half_gap[last][:, cols], ACT.Tanh)
-        for cols in halves:
+            nc.vector.scalar_tensor_tensor(half_gap[last][:, cols], third_last[h][:], 0.25, y[last][:, cols], ALU.mult, ALU.mult)
+            nc.scalar.activation(slope[last][:, cols], half_gap[last][:, cols], ACT.Tanh, scale=0.5)
             nc.scalar.activation(small[:, small_at[last]][:, cols], slope[last][:, cols], ACT.Abs)
 
         second = keep.tile([P, TILES, S], F32, name="second", tag="second", align_bytes=64)
@@ -211,56 +221,59 @@ def tile_picked_softarg_none_p_kernel(
         cut = 2 * S - P
         nc.scalar.activation(soft[:, :cut], small[:, :cut], ACT.Ln, bias=1.0)
         nc.scalar.activation(soft[:, cut:], small[:, cut:], ACT.Ln, bias=1.0)
-        for t in (0, 1, last):
+
+        def gather_second(t):
             gather(second[:, t, :], t, c2_list)
+
+        gather_second(0)
+        gather_second(1)
+        times_y(s12[0], second[:, 0, :], 0, -0.25)
+        gather_second(2)
+        gather_second(last)
         nc.gpsimd.tensor_tensor(s12[last][:], second[:, last, :], eighth_y[last][:], ALU.mult)
-        for t in range(2):
+        for t in (1, 2):
             times_y(s12[t], second[:, t, :], t, -0.25)
-        half_lead = sb("half_lead")
-        nc.vector.scalar_tensor_tensor(half_lead[:], half_gap[last][:], 0.0, s12[last][:], ALU.max, ALU.subtract)
-        late_second = sb("late_second", tag="small")
-        gather(late_second[:, halves[0]], 2, c2_list, halves[0])
-        half_whole = sb("half_whole")
-        nc.vector.scalar_tensor_tensor(half_whole[:], soft[:, small_at[last]], -0.5, half_lead[:], ALU.mult, ALU.add)
-        gather(late_second[:, halves[1]], 2, c2_list, halves[1])
-        for cols in halves:
-            times_y(s12[2], late_second, 2, -0.25, cols)
+        top = [sb("top%d" % h, HALF) for h in range(2)]
+        whole = [sb("whole%d" % h, HALF) for h in range(2)]
+        for h, cols in enumerate(halves):
+            nc.vector.scalar_tensor_tensor(top[h][:], half_gap[last][:, cols], 0.0, s12[last][:, cols], ALU.max, ALU.subtract)
+        for h, engine in enumerate((nc.vector, nc.gpsimd)):
+            engine.tensor_tensor(whole[h][:], top[h][:], soft[:, small_at[last]][:, halves[h]], ALU.subtract)
         turn(lead[0][:], s12[0][:])
         turn(lead[0][:], soft[:, small_at[0]], closes=True)
-        turn(lead[1][:], s12[1][:])
-        turn(lead[1][:], soft[:, small_at[1]], closes=True)
-        turn(lead[2][:], soft[:, small_at[2]])
-        turn(lead[2][:], s12[2][:], closes=True)
+        for t in (1, 2):
+            turn(lead[t][:], soft[:, small_at[t]])
+        for t in (1, 2):
+            turn(lead[t][:], s12[t][:], closes=True)
 
         rows = out.rearrange("(p t) j -> p t j", t=TILES)
-        pieces = [(last, slice(0, S), None)] + [
+        pieces = [
             (n // 2, halves[n % 2], bank) for n, bank in enumerate(("y0", "y1", "y3", "a2", "a0", "y2"))
-        ]
+        ] + [(last, cols, None) for cols in halves]
         outer = []
         for n, (t, cols, bank) in enumerate(pieces):
-            width = cols.stop - cols.start
             if t == last:
-                outer.append(sb("outer%d" % n))
-                nc.scalar.activation(outer[n][:], half_whole[:], ACT.Tanh, bias=0.5 * math.log(2.0))
+                outer.append(sb("outer%d" % n, HALF))
+                nc.scalar.activation(outer[n][:], whole[n % 2][:], ACT.Tanh, bias=0.5 * math.log(2.0), scale=0.5)
             else:
-                outer_turned = sb("outer_turned%d" % n, width)
+                outer_turned = sb("outer_turned%d" % n, HALF)
                 nc.scalar.activation(outer_turned[:], lead[t][:, cols], ACT.Tanh, scale=0.5)
-                outer.append(psum.tile([P, width], F32, name="outer%d" % n, tag=bank))
+                outer.append(psum.tile([P, HALF], F32, name="outer%d" % n, tag=bank))
                 turn(outer[n][:], outer_turned[:], opens=True, closes=True)
-        shift = [sb("shift%d" % t) for t in range(TILES)]
-        result = [sb("result%d" % t) for t in range(TILES)]
+        shift = [sb("shift%d" % n, HALF, tag="s12_3" if n == 0 else None) for n in range(len(pieces))]
 
-        def finish(engine, t, cols):
-            engine.tensor_scalar(result[t][:, cols], shift[t][:, cols], 0.5, 1.0, ALU.mult, ALU.add)
+        def finish(n):
+            t, cols, bank = pieces[n]
+            result = sb("result%d" % n, HALF, tag={1: "top1", 2: "whole1"}.get(n))
+            if n in (0, 1, len(pieces) - 1):
+                engine = nc.gpsimd if n == 1 else nc.vector
+                engine.tensor_scalar(result[:], shift[n][:], 0.5, 1.0, ALU.mult, ALU.add)
+            else:
+                nc.scalar.activation(result[:], shift[n][:], ACT.Identity, bias=1.0, scale=0.5)
+            nc.sync.dma_start(rows[:, t, cols], result[:])
 
         for n, (t, cols, bank) in enumerate(pieces):
-            nc.vector.scalar_tensor_tensor(shift[t][:, cols], outer[n][:], 1.0, slope[t][:, cols], ALU.add, ALU.mult)
-        finish(nc.gpsimd, last, slice(0, S))
-        nc.sync.dma_start(rows[:, last, :], result[last][:])
-        for t in range(2):
-            finish(nc.gpsimd, t, halves[0])
-            nc.scalar.activation(result[t][:, halves[1]], shift[t][:, halves[1]], ACT.Identity, bias=1.0, scale=0.5)
-            nc.sync.dma_start(rows[:, t, :], result[t][:])
-        for cols in halves:
-            finish(nc.vector, 2, cols)
-            nc.sync.dma_start(rows[:, 2, cols], result[2][:, cols])
+            nc.vector.scalar_tensor_tensor(shift[n][:], outer[n][:], 1.0, slope[t][:, cols], ALU.add, ALU.mult)
+            if n > 0:
+                finish(n - 1)
+        finish(len(pieces) - 1)

@@ -20,8 +20,12 @@ ACT = mybir.ActivationFunctionType
 P = 128
 PACK = 4
 TILES = N // P
+LAST = TILES - 1
 HALF = S // 2
-WINDOW = 2 * S
+WIDE = 2 * S
+ROW_BYTES = S * 4
+STRIPE = 16
+GPSIMD_HALVES = 3
 
 
 def tile_picked_softarg_none_p_kernel(
@@ -32,14 +36,22 @@ def tile_picked_softarg_none_p_kernel(
         lists = ctx.enter_context(tc.tile_pool(name="lists", bufs=1))
         keep = ctx.enter_context(tc.tile_pool(name="keep", bufs=1))
         psum = ctx.enter_context(tc.psum_pool(name="psum", bufs=1))
+        halves = [slice(0, HALF), slice(HALF, S)]
+        whole = slice(0, S)
 
         def load_list(name, dram):
-            tile = lists.tile([P, S // 16], U16, name=name)
+            tile = lists.tile([P, S // STRIPE], U16, name=name)
             nc.sync.dma_start(tile[:], dram)
             return tile
 
-        def sb(name, width=S, tag=None):
+        def entries(cols):
+            return slice(cols.start // STRIPE, cols.stop // STRIPE)
+
+        def row(name, width=S, tag=None):
             return keep.tile([P, width], F32, name=name, tag=tag or name, align_bytes=64)
+
+        def blocks(values, which=slice(0, 2)):
+            return values.rearrange("p (b c) -> p b c", c=P)[:, which, :]
 
         def turn(bank, term, opens=False, closes=False):
             count = term.shape[1] // P
@@ -50,18 +62,16 @@ def tile_picked_softarg_none_p_kernel(
                     start=opens and b == 0, stop=closes and b == count - 1, is_transpose=True,
                 )
 
-        def pick(name, table, dtype, offsets, tag=None):
-            picked = keep.tile([P, S], dtype, name=name, tag=tag or name, align_bytes=64)
-            nc.vector.tensor_copy(picked[:], table[:].indirect(offsets[:]))
+        def pick_scales(name, offsets):
+            picked = keep.tile([P, S], U8, name=name, align_bytes=64)
+            nc.vector.tensor_copy(picked[:], table_scales[:].indirect(offsets[:]))
             return picked
 
-        def interleave_pair(name, whole, pair, copy):
-            grouped = keep.tile([P, 2, P, PACK], BF16, name=name, tag=name, align_bytes=64)
+        def round_half(copy, grouped, raw, h):
             copy(
-                grouped[:].rearrange("p t m j -> p m j t"),
-                whole.rearrange("p j (m t) -> p m j t", t=TILES)[:, :, :, 2 * pair : 2 * pair + 2],
+                grouped[:, :, h * P // 2 : (h + 1) * P // 2, :].rearrange("p t m j -> p m j t"),
+                raw[:, :, h * N // 2 : (h + 1) * N // 2].rearrange("p j (m t) -> p m j t", t=TILES),
             )
-            return grouped
 
         def quantise(name, grouped):
             count = grouped.shape[1]
@@ -72,13 +82,13 @@ def tile_picked_softarg_none_p_kernel(
             )
             return [(words, scales, slice(i * P, (i + 1) * P)) for i in range(count)]
 
-        def project(name, weight, picked, bank, tokens=slice(0, S)):
-            cols = weight[2]
+        def project(name, weight, picked, bank, tokens=whole):
+            words, scales, cols = weight
             acc = psum.tile([P, tokens.stop - tokens.start], F32, name=name, tag=bank)
             nc.tensor.matmul_mx(
                 out=acc[:],
-                lhsT=weight[0][:, cols].bitcast(FP8X4),
-                lhsT_scale=weight[1][:, cols],
+                lhsT=words[:, cols].bitcast(FP8X4),
+                lhsT_scale=scales[:, cols],
                 rhs=picked[0][:, tokens].bitcast(FP8X4),
                 rhs_scale=picked[1][:, tokens],
                 start=True,
@@ -86,12 +96,8 @@ def tile_picked_softarg_none_p_kernel(
             )
             return acc
 
-        def entries(cols):
-            return slice(cols.start // 16, cols.stop // 16)
-
-        halves = [slice(0, HALF), slice(HALF, S)]
         table_scales = keep.tile([P, T], U8, name="table_scales")
-        nc.vector.memset(table_scales[:].bitcast(I32), 0)
+        nc.gpsimd.memset(table_scales[:].bitcast(I32), 0)
         ref_list = load_list("ref_list", ref)
         offs_list = load_list("offs_list", offs)
         for q in range(4):
@@ -100,145 +106,145 @@ def tile_picked_softarg_none_p_kernel(
                 x_scales[0, 4 * q : 4 * q + 4, :].bitcast(I32),
             )
         shared = ctx.enter_context(tc.tile_pool(name="shared", bufs=1))
-        w2_whole = shared.tile([P, PACK, N], F32, name="w2_whole", offset=0)[:]
-        w1_whole = shared.tile([P, PACK, N], F32, name="w1_whole", offset=2 * WINDOW * 4)[:]
-        windows = [shared.tile([P, WINDOW], F32, name="window%d" % t, offset=(0, 2, 3, 1)[t] * WINDOW * 4) for t in range(TILES)]
-        nc.sync.dma_start(w2_whole, w2.rearrange("(p j) c -> p j c", j=PACK))
+        w2_raw = shared.tile([P, PACK, N], F32, name="w2_raw", offset=0)[:]
+        w1_raw = shared.tile([P, PACK, N], F32, name="w1_raw", offset=4 * ROW_BYTES)[:]
+        windows = [
+            shared.tile([P, width], F32, name="window%d" % t, offset=first_row * ROW_BYTES)
+            for t, (width, first_row) in enumerate(((S, 0), (WIDE, 4), (WIDE, 6), (WIDE, 2)))
+        ]
+        nc.sync.dma_start(w2_raw, w2.rearrange("(p j) c -> p j c", j=PACK))
         table_words = keep.tile([P, T], U32, name="table_words")
         nc.sync.dma_start(
             table_words[:].bitcast(I32), x_words[0].rearrange("p n t -> p (n t)").bitcast(I32)
         )
         c1_list = load_list("c1_list", c1)
         c3_list = load_list("c3_list", c3)
-        nc.sync.dma_start(w1_whole, w1.rearrange("(p j) c -> p j c", j=PACK))
+        nc.sync.dma_start(w1_raw, w1.rearrange("(p j) c -> p j c", j=PACK))
         c2_list = load_list("c2_list", c2)
         identity = keep.tile([P, P], F32, name="identity")
         make_identity(nc, identity[:])
 
-        right_scales = pick("right_scales", table_scales, U8, ref_list)
-        left_scales = pick("left_scales", table_scales, U8, offs_list)
-        w2_low = interleave_pair("w2_low", w2_whole, 0, nc.vector.tensor_copy)
-        w2_high = interleave_pair("w2_high", w2_whole, 1, nc.scalar.copy)
-        w2_q = quantise("w2_low", w2_low[:]) + quantise("w2_high", w2_high[:])
-        right_words = keep.tile([P, S], U32, name="right_words", tag="w2_low", align_bytes=64)
+        right_scales = pick_scales("right_scales", ref_list)
+        left_scales = pick_scales("left_scales", offs_list)
+        w2_grouped = keep.tile([P, TILES, P, PACK], BF16, name="w2_grouped", tag="w2_grouped", align_bytes=64)
+        round_half(nc.vector.tensor_copy, w2_grouped, w2_raw, 0)
+        round_half(nc.scalar.copy, w2_grouped, w2_raw, 1)
+        w2_q = quantise("w2_low", w2_grouped[:, 0:2]) + quantise("w2_high", w2_grouped[:, 2:4])
+        right_words = shared.tile([P, S], U32, name="right_words", offset=ROW_BYTES, align_bytes=64)
+        left_words = keep.tile([P, S], U32, name="left_words", tag="w2_grouped", align_bytes=64)
         for cols in halves:
             nc.vector.tensor_copy(right_words[:, cols], table_words[:].indirect(ref_list[:, entries(cols)]))
+        nc.vector.tensor_copy(left_words[:], table_words[:].indirect(offs_list[:]))
         right = (right_words, right_scales)
-        left = (pick("left_words", table_words, U32, offs_list, tag="w2_high"), left_scales)
+        left = (left_words, left_scales)
 
-        last = TILES - 1
         w1_grouped = keep.tile([P, TILES, P, PACK], BF16, name="w1_grouped", align_bytes=64)
-
-        def round_w1(h):
-            nc.scalar.copy(
-                w1_grouped[:, :, h * P // 2 : (h + 1) * P // 2, :].rearrange("p t m j -> p m j t"),
-                w1_whole[:, :, h * N // 2 : (h + 1) * N // 2].rearrange("p j (m t) -> p m j t", t=TILES),
-            )
-
-        def fill(t, bank):
-            nc.scalar.copy(windows[t][:, :S], project("e%d" % t, w2_q[t], right, bank)[:])
-
-        first = {t: sb("first%d" % t) for t in range(last)}
-        third = {t: sb("third%d" % t) for t in range(last)}
-        half_gap = [sb("half_gap%d" % t) for t in range(TILES)]
-        size = [sb("size%d" % t) for t in range(TILES)]
-        small = sb("small", TILES * S)
-        small_at = [slice(0, S), slice(2 * S, 3 * S), slice(3 * S, 4 * S), slice(S, 2 * S)]
-        lead = {}
+        first = {t: row("first%d" % t) for t in range(LAST)}
+        third = {t: row("third%d" % t) for t in range(LAST)}
+        half_gap = [row("half_gap%d" % t) for t in range(LAST)]
+        last_gap = row("last_gap")
+        size = [row("size%d" % t) for t in range(LAST)]
         slope = {}
+        lead = {}
+        small = row("small", TILES * S)
+        small_at = [slice(P, P + S), slice(P + S, P + 2 * S), slice(3 * S, 4 * S)]
+        last_at = [slice(10, 12), slice(0, 10, 9)]
 
-        def gather_first(t, parts=(slice(0, S),)):
+        def gather_first(t, parts):
             for cols in parts:
                 nc.vector.tensor_copy(first[t][:, cols], windows[t][:].indirect(c1_list[:, entries(cols)]))
 
-        def gather(dest, t, offsets, cols=slice(0, S)):
-            nc.vector.tensor_tensor(dest, windows[t][:].indirect(offsets[:, entries(cols)]), first[t][:, cols], ALU.subtract)
+        def gather_less_first(dest, t, offsets, cols=whole):
+            nc.vector.tensor_tensor(
+                dest, windows[t][:].indirect(offsets[:, entries(cols)]), first[t][:, cols], ALU.subtract
+            )
 
-        def shape(n, t, cols, bank):
-            nc.scalar.activation(size[t][:, cols], half_gap[t][:, cols], ACT.Abs)
-            slope[n] = sb("slope%d" % n, cols.stop - cols.start)
-            nc.scalar.activation(slope[n][:], half_gap[t][:, cols], ACT.Tanh)
-            nc.scalar.activation(small[:, small_at[n]], size[t][:, cols], ACT.Exp, scale=-2.0)
-            lead[n] = psum.tile([P, cols.stop - cols.start], F32, name="lead%d" % n, tag=bank)
-            turn(lead[n][:], half_gap[t][:, cols], opens=True)
-            turn(lead[n][:], size[t][:, cols])
-
-        def times_y(dest, src, t, scale, cols=slice(0, S)):
+        def times_y(dest, src, t, scale, cols=whole):
             nc.vector.scalar_tensor_tensor(dest[:, cols], src[:, cols], scale, y[t][:, cols], ALU.mult, ALU.mult)
+
+        def open_lead(t, bank):
+            lead[t] = psum.tile([P, S], F32, name="lead%d" % t, tag=bank)
+            turn(lead[t][:], half_gap[t][:], opens=True)
+            turn(lead[t][:], size[t][:])
+
+        def shape(t, bank):
+            nc.scalar.activation(size[t][:], half_gap[t][:], ACT.Abs)
+            slope[t] = row("slope%d" % t)
+            nc.scalar.activation(slope[t][:], half_gap[t][:], ACT.Tanh)
+            nc.scalar.activation(small[:, small_at[t]], size[t][:], ACT.Exp, scale=-2.0)
+            open_lead(t, bank)
 
         e0 = [project("e0_%d" % h, w2_q[0], right, "a%d" % h, halves[h]) for h in range(2)]
         for h in range(2):
             nc.scalar.copy(windows[0][:, halves[h]], e0[h][:])
-        round_w1(0)
-        round_w1(1)
-        for t in range(1, TILES):
-            fill(t, "a%d" % (2 + (t + 1) % 2))
+        for h in range(2):
+            round_half(nc.scalar.copy, w1_grouped, w1_raw, h)
+        for t, bank in ((1, "a2"), (2, "a3"), (LAST, "a2")):
+            nc.scalar.copy(windows[t][:, :S], project("e%d" % t, w2_q[t], right, bank)[:])
         gather_first(0, halves)
         for cols in halves:
-            gather(third[0][:, cols], 0, c3_list, cols)
+            gather_less_first(third[0][:, cols], 0, c3_list, cols)
         w1_q = quantise("w1_low", w1_grouped[:, 0:2]) + quantise("w1_high", w1_grouped[:, 2:4])
         y = [project("y%d" % t, w1_q[t], left, "y%d" % t) for t in range(TILES)]
-        gather_first(1)
+        gather_first(1, [whole])
         times_y(half_gap[0], third[0], 0, 0.125)
-        eighth_y = {t: sb("eighth_y%d" % t) for t in range(1, TILES)}
+        eighth_y = {t: row("eighth_y%d" % t) for t in (1, 2)}
+        last_quarter_y = row("last_quarter_y")
         for t in (1, 2):
             nc.scalar.activation(eighth_y[t][:], y[t][:], ACT.Copy, scale=0.125)
-        shape(0, 0, slice(0, S), "a0")
-        nc.scalar.activation(eighth_y[last][:], y[last][:], ACT.Copy, scale=0.25)
-        gather(third[1][:], 1, c3_list)
+        shape(0, "a0")
+        nc.scalar.activation(last_quarter_y[:], y[LAST][:], ACT.Copy, scale=0.25)
+        gather_less_first(third[1][:], 1, c3_list)
         nc.gpsimd.tensor_tensor(half_gap[1][:], third[1][:], eighth_y[1][:], ALU.mult)
         gather_first(2, halves)
-        shape(1, 1, slice(0, S), "a1")
+        shape(1, "a1")
         for cols in halves:
-            gather(third[2][:, cols], 2, c3_list, cols)
-        first[last] = sb("first3", tag="third1")
-        gather_first(last, halves)
-        slope[2] = sb("slope2")
-        lead[2] = psum.tile([P, S], F32, name="lead2", tag="a3")
-        for n, blocks in enumerate((slice(1, 3), slice(0, 4, 3))):
-            def part(tile, blocks=blocks):
-                return tile.rearrange("p (b c) -> p b c", c=P)[:, blocks, :]
-            nc.gpsimd.tensor_tensor(part(half_gap[2][:]), part(third[2][:]), part(eighth_y[2][:]), ALU.mult)
-            nc.scalar.activation(part(size[2][:]), part(half_gap[2][:]), ACT.Abs)
-            nc.scalar.activation(part(small[:, small_at[2]]), part(size[2][:]), ACT.Exp, scale=-2.0)
-            nc.scalar.activation(part(slope[2][:]), part(half_gap[2][:]), ACT.Tanh)
-            for term in (half_gap[2], size[2]):
-                for k in range(4)[blocks]:
-                    cols = slice(k * P, (k + 1) * P)
-                    turn(lead[2][:, cols], term[:, cols], opens=n == 0 and k == 1 and term is half_gap[2])
-        third_last = [sb("third3_0", HALF, tag="second"), sb("third3_1", HALF, tag="third3_1")]
+            gather_less_first(third[2][:, cols], 2, c3_list, cols)
+        nc.gpsimd.tensor_tensor(half_gap[2][:], third[2][:], eighth_y[2][:], ALU.mult)
+        first[LAST] = row("first3", tag="third1")
+        gather_first(LAST, halves)
+        for cols in halves:
+            nc.scalar.activation(size[2][:, cols], half_gap[2][:, cols], ACT.Abs)
+        for cols in halves:
+            nc.scalar.activation(small[:, small_at[2]][:, cols], size[2][:, cols], ACT.Exp, scale=-2.0)
+        open_lead(2, "a3")
+        last_third = [row("third3_0", HALF, tag="second"), row("third3_1", HALF)]
         for h, cols in enumerate(halves):
-            gather(third_last[h][:], last, c3_list, cols)
-        slope[last] = sb("slope3")
+            gather_less_first(last_third[h][:], LAST, c3_list, cols)
+        slope[LAST] = row("slope3")
         for h, cols in enumerate(halves):
-            nc.vector.scalar_tensor_tensor(half_gap[last][:, cols], third_last[h][:], 0.25, y[last][:, cols], ALU.mult, ALU.mult)
-            nc.scalar.activation(slope[last][:, cols], half_gap[last][:, cols], ACT.Tanh, scale=0.5)
-            nc.scalar.activation(small[:, small_at[last]][:, cols], slope[last][:, cols], ACT.Abs)
+            nc.vector.scalar_tensor_tensor(
+                last_gap[:, cols], last_third[h][:], 0.25, y[LAST][:, cols], ALU.mult, ALU.mult
+            )
+            nc.scalar.activation(slope[LAST][:, cols], last_gap[:, cols], ACT.Tanh, scale=0.5)
+        for h, cols in enumerate(halves):
+            nc.scalar.activation(blocks(small[:], last_at[h]), blocks(slope[LAST][:, cols]), ACT.Abs)
 
         second = keep.tile([P, TILES, S], F32, name="second", tag="second", align_bytes=64)
-        s12 = [sb("s12_%d" % t) for t in range(TILES)]
-        soft = sb("soft", TILES * S)
-        cut = 2 * S - P
-        nc.scalar.activation(soft[:, :cut], small[:, :cut], ACT.Ln, bias=1.0)
-        nc.scalar.activation(soft[:, cut:], small[:, cut:], ACT.Ln, bias=1.0)
-
-        def gather_second(t):
-            gather(second[:, t, :], t, c2_list)
-
-        gather_second(0)
-        gather_second(1)
+        s12 = [row("s12_%d" % t) for t in range(LAST)]
+        last_s21 = row("last_s21")
+        soft = row("soft", TILES * S)
+        for run in (slice(0, 2 * S), slice(2 * S, 4 * S)):
+            nc.scalar.activation(soft[:, run], small[:, run], ACT.Ln, bias=1.0)
+        for cols in halves:
+            gather_less_first(second[:, 0, cols], 0, c2_list, cols)
+        gather_less_first(second[:, 1, :], 1, c2_list)
         times_y(s12[0], second[:, 0, :], 0, -0.25)
-        gather_second(2)
-        gather_second(last)
-        nc.gpsimd.tensor_tensor(s12[last][:], second[:, last, :], eighth_y[last][:], ALU.mult)
-        for t in (1, 2):
-            times_y(s12[t], second[:, t, :], t, -0.25)
-        top = [sb("top%d" % h, HALF) for h in range(2)]
-        whole = [sb("whole%d" % h, HALF) for h in range(2)]
+        for t in (2, LAST):
+            gather_less_first(second[:, t, :], t, c2_list)
+        nc.gpsimd.tensor_tensor(last_s21[:], second[:, LAST, :], last_quarter_y[:], ALU.mult)
+        times_y(s12[1], second[:, 1, :], 1, -0.25)
+        for cols in halves:
+            times_y(s12[2], second[:, 2, :], 2, -0.25, cols)
+        last_top = [row("last_top%d" % h, HALF) for h in range(2)]
+        last_lead = [row("last_lead%d" % h, HALF) for h in range(2)]
         for h, cols in enumerate(halves):
-            nc.vector.scalar_tensor_tensor(top[h][:], half_gap[last][:, cols], 0.0, s12[last][:, cols], ALU.max, ALU.subtract)
-        for h, engine in enumerate((nc.vector, nc.gpsimd)):
-            engine.tensor_tensor(whole[h][:], top[h][:], soft[:, small_at[last]][:, halves[h]], ALU.subtract)
+            nc.vector.scalar_tensor_tensor(
+                blocks(last_top[h][:]), blocks(last_gap[:, cols]), 0.0, blocks(soft[:], last_at[h]),
+                ALU.max, ALU.subtract,
+            )
+        for h, cols in enumerate(halves):
+            nc.vector.tensor_tensor(last_lead[h][:], last_top[h][:], last_s21[:, cols], ALU.subtract)
         turn(lead[0][:], s12[0][:])
         turn(lead[0][:], soft[:, small_at[0]], closes=True)
         for t in (1, 2):
@@ -246,34 +252,30 @@ def tile_picked_softarg_none_p_kernel(
         for t in (1, 2):
             turn(lead[t][:], s12[t][:], closes=True)
 
-        rows = out.rearrange("(p t) j -> p t j", t=TILES)
-        pieces = [
-            (n // 2, halves[n % 2], bank) for n, bank in enumerate(("y0", "y1", "y3", "a2", "a0", "y2"))
-        ] + [(last, cols, None) for cols in halves]
+        turned = [(n // 2, n % 2) for n in range(2 * LAST)]
+        pieces = turned + [(LAST, h) for h in range(2)]
         outer = []
-        for n, (t, cols, bank) in enumerate(pieces):
-            if t == last:
-                outer.append(sb("outer%d" % n, HALF))
-                nc.scalar.activation(outer[n][:], whole[n % 2][:], ACT.Tanh, bias=0.5 * math.log(2.0), scale=0.5)
-            else:
-                outer_turned = sb("outer_turned%d" % n, HALF)
-                nc.scalar.activation(outer_turned[:], lead[t][:, cols], ACT.Tanh, scale=0.5)
-                outer.append(psum.tile([P, HALF], F32, name="outer%d" % n, tag=bank))
-                turn(outer[n][:], outer_turned[:], opens=True, closes=True)
-        shift = [sb("shift%d" % n, HALF, tag="s12_3" if n == 0 else None) for n in range(len(pieces))]
-
-        def finish(n):
-            t, cols, bank = pieces[n]
-            result = sb("result%d" % n, HALF, tag={1: "top1", 2: "whole1"}.get(n))
-            if n in (0, 1, len(pieces) - 1):
-                engine = nc.gpsimd if n == 1 else nc.vector
-                engine.tensor_scalar(result[:], shift[n][:], 0.5, 1.0, ALU.mult, ALU.add)
-            else:
+        for n, bank in enumerate(("y0", "y1", "y3", "a2", "a0", "y2")):
+            t, h = turned[n]
+            outer_turned = row("outer_turned%d" % n, HALF)
+            nc.scalar.activation(outer_turned[:], lead[t][:, halves[h]], ACT.Tanh, scale=0.5)
+            outer.append(psum.tile([P, HALF], F32, name="outer%d" % n, tag=bank))
+            turn(outer[n][:], outer_turned[:], opens=True, closes=True)
+        slope[2] = row("slope2", tag="outer_turned0")
+        nc.scalar.activation(slope[2][:], half_gap[2][:], ACT.Tanh)
+        for h in range(2):
+            outer.append(row("last_outer%d" % h, HALF))
+            nc.scalar.activation(outer[-1][:], last_lead[h][:], ACT.Tanh, bias=0.5 * math.log(2.0), scale=0.5)
+        shift = [row("shift0", HALF, tag="last_top0")] + [row("shift%d" % n, HALF) for n in range(1, len(pieces))]
+        for n, (t, h) in enumerate(pieces):
+            nc.vector.scalar_tensor_tensor(shift[n][:], outer[n][:], 1.0, slope[t][:, halves[h]], ALU.add, ALU.mult)
+        rows = out.rearrange("(p t) j -> p t j", t=TILES)
+        for n, (t, h) in enumerate(pieces):
+            result = row("result%d" % n, HALF, tag="last_lead1" if n == GPSIMD_HALVES else None)
+            if n < GPSIMD_HALVES:
+                nc.gpsimd.tensor_scalar(result[:], shift[n][:], 0.5, 1.0, ALU.mult, ALU.add)
+            elif t < LAST:
                 nc.scalar.activation(result[:], shift[n][:], ACT.Identity, bias=1.0, scale=0.5)
-            nc.sync.dma_start(rows[:, t, cols], result[:])
-
-        for n, (t, cols, bank) in enumerate(pieces):
-            nc.vector.scalar_tensor_tensor(shift[n][:], outer[n][:], 1.0, slope[t][:, cols], ALU.add, ALU.mult)
-            if n > 0:
-                finish(n - 1)
-        finish(len(pieces) - 1)
+            else:
+                nc.vector.tensor_scalar(result[:], shift[n][:], 0.5, 1.0, ALU.mult, ALU.add)
+            nc.sync.dma_start(rows[:, t, halves[h]], result[:])

import math
from contextlib import ExitStack

import concourse.mybir as mybir
from concourse.masks import make_identity

K, T, S, N = 512, 2048, 512, 512
FLOPS = 2 * 2 * K * N * S

F32 = mybir.dt.float32
BF16 = mybir.dt.bfloat16
I32 = mybir.dt.int32
U32 = mybir.dt.uint32
U16 = mybir.dt.uint16
U8 = mybir.dt.uint8
FP8X4 = mybir.dt.float8_e4m3fn_x4
ALU = mybir.AluOpType
ACT = mybir.ActivationFunctionType

P = 128
PACK = 4
TILES = N // P
LAST = TILES - 1
HALF = S // 2
WIDE = 2 * S
ROW_BYTES = S * 4
STRIPE = 16
GPSIMD_HALVES = 3


def tile_picked_softarg_none_p_kernel(
    tc, x_words, x_scales, w1, w2, offs, ref, c1, c2, c3, out
):
    nc = tc.nc
    with ExitStack() as ctx:
        lists = ctx.enter_context(tc.tile_pool(name="lists", bufs=1))
        keep = ctx.enter_context(tc.tile_pool(name="keep", bufs=1))
        psum = ctx.enter_context(tc.psum_pool(name="psum", bufs=1))
        halves = [slice(0, HALF), slice(HALF, S)]
        whole = slice(0, S)

        def load_list(name, dram):
            tile = lists.tile([P, S // STRIPE], U16, name=name)
            nc.sync.dma_start(tile[:], dram)
            return tile

        def entries(cols):
            return slice(cols.start // STRIPE, cols.stop // STRIPE)

        def row(name, width=S, tag=None):
            return keep.tile([P, width], F32, name=name, tag=tag or name, align_bytes=64)

        def blocks(values, which=slice(0, 2)):
            return values.rearrange("p (b c) -> p b c", c=P)[:, which, :]

        def turn(bank, term, opens=False, closes=False):
            count = term.shape[1] // P
            for b in range(count):
                cols = slice(b * P, (b + 1) * P)
                nc.tensor.matmul(
                    bank[:, cols], term[:, cols], identity[:],
                    start=opens and b == 0, stop=closes and b == count - 1, is_transpose=True,
                )

        def pick_scales(name, offsets):
            picked = keep.tile([P, S], U8, name=name, align_bytes=64)
            nc.vector.tensor_copy(picked[:], table_scales[:].indirect(offsets[:]))
            return picked

        def round_half(copy, grouped, raw, h):
            copy(
                grouped[:, :, h * P // 2 : (h + 1) * P // 2, :].rearrange("p t m j -> p m j t"),
                raw[:, :, h * N // 2 : (h + 1) * N // 2].rearrange("p j (m t) -> p m j t", t=TILES),
            )

        def quantise(name, grouped):
            count = grouped.shape[1]
            words = keep.tile([P, count * P], U32, name=name + "_words", align_bytes=64)
            scales = keep.tile([P, count * P], U8, name=name + "_scales", align_bytes=64)
            nc.vector.quantize_mx(
                out=words[:].bitcast(FP8X4), scales=scales[:], in_=grouped.rearrange("p t m j -> p (t m j)")
            )
            return [(words, scales, slice(i * P, (i + 1) * P)) for i in range(count)]

        def project(name, weight, picked, bank, tokens=whole):
            words, scales, cols = weight
            acc = psum.tile([P, tokens.stop - tokens.start], F32, name=name, tag=bank)
            nc.tensor.matmul_mx(
                out=acc[:],
                lhsT=words[:, cols].bitcast(FP8X4),
                lhsT_scale=scales[:, cols],
                rhs=picked[0][:, tokens].bitcast(FP8X4),
                rhs_scale=picked[1][:, tokens],
                start=True,
                stop=True,
            )
            return acc

        table_scales = keep.tile([P, T], U8, name="table_scales")
        nc.gpsimd.memset(table_scales[:].bitcast(I32), 0)
        ref_list = load_list("ref_list", ref)
        offs_list = load_list("offs_list", offs)
        for q in range(4):
            nc.sync.dma_start(
                table_scales[32 * q : 32 * q + 4, :].bitcast(I32),
                x_scales[0, 4 * q : 4 * q + 4, :].bitcast(I32),
            )
        shared = ctx.enter_context(tc.tile_pool(name="shared", bufs=1))
        w2_raw = shared.tile([P, PACK, N], F32, name="w2_raw", offset=0)[:]
        w1_raw = shared.tile([P, PACK, N], F32, name="w1_raw", offset=4 * ROW_BYTES)[:]
        windows = [
            shared.tile([P, width], F32, name="window%d" % t, offset=first_row * ROW_BYTES)
            for t, (width, first_row) in enumerate(((S, 0), (WIDE, 4), (WIDE, 6), (WIDE, 2)))
        ]
        nc.sync.dma_start(w2_raw, w2.rearrange("(p j) c -> p j c", j=PACK))
        table_words = keep.tile([P, T], U32, name="table_words")
        nc.sync.dma_start(
            table_words[:].bitcast(I32), x_words[0].rearrange("p n t -> p (n t)").bitcast(I32)
        )
        c1_list = load_list("c1_list", c1)
        c3_list = load_list("c3_list", c3)
        nc.sync.dma_start(w1_raw, w1.rearrange("(p j) c -> p j c", j=PACK))
        c2_list = load_list("c2_list", c2)
        identity = keep.tile([P, P], F32, name="identity")
        make_identity(nc, identity[:])

        right_scales = pick_scales("right_scales", ref_list)
        left_scales = pick_scales("left_scales", offs_list)
        w2_grouped = keep.tile([P, TILES, P, PACK], BF16, name="w2_grouped", tag="w2_grouped", align_bytes=64)
        round_half(nc.vector.tensor_copy, w2_grouped, w2_raw, 0)
        round_half(nc.scalar.copy, w2_grouped, w2_raw, 1)
        w2_q = quantise("w2_low", w2_grouped[:, 0:2]) + quantise("w2_high", w2_grouped[:, 2:4])
        right_words = shared.tile([P, S], U32, name="right_words", offset=ROW_BYTES, align_bytes=64)
        left_words = keep.tile([P, S], U32, name="left_words", tag="w2_grouped", align_bytes=64)
        for cols in halves:
            nc.vector.tensor_copy(right_words[:, cols], table_words[:].indirect(ref_list[:, entries(cols)]))
        nc.vector.tensor_copy(left_words[:], table_words[:].indirect(offs_list[:]))
        right = (right_words, right_scales)
        left = (left_words, left_scales)

        w1_grouped = keep.tile([P, TILES, P, PACK], BF16, name="w1_grouped", align_bytes=64)
        first = {t: row("first%d" % t) for t in range(LAST)}
        third = {t: row("third%d" % t) for t in range(LAST)}
        half_gap = [row("half_gap%d" % t) for t in range(LAST)]
        last_gap = row("last_gap")
        size = [row("size%d" % t) for t in range(LAST)]
        slope = {}
        lead = {}
        small = row("small", TILES * S)
        small_at = [slice(P, P + S), slice(P + S, P + 2 * S), slice(3 * S, 4 * S)]
        last_at = [slice(10, 12), slice(0, 10, 9)]

        def gather_first(t, parts):
            for cols in parts:
                nc.vector.tensor_copy(first[t][:, cols], windows[t][:].indirect(c1_list[:, entries(cols)]))

        def gather_less_first(dest, t, offsets, cols=whole):
            nc.vector.tensor_tensor(
                dest, windows[t][:].indirect(offsets[:, entries(cols)]), first[t][:, cols], ALU.subtract
            )

        def times_y(dest, src, t, scale, cols=whole):
            nc.vector.scalar_tensor_tensor(dest[:, cols], src[:, cols], scale, y[t][:, cols], ALU.mult, ALU.mult)

        def open_lead(t, bank):
            lead[t] = psum.tile([P, S], F32, name="lead%d" % t, tag=bank)
            turn(lead[t][:], half_gap[t][:], opens=True)
            turn(lead[t][:], size[t][:])

        def shape(t, bank):
            nc.scalar.activation(size[t][:], half_gap[t][:], ACT.Abs)
            slope[t] = row("slope%d" % t)
            nc.scalar.activation(slope[t][:], half_gap[t][:], ACT.Tanh)
            nc.scalar.activation(small[:, small_at[t]], size[t][:], ACT.Exp, scale=-2.0)
            open_lead(t, bank)

        e0 = [project("e0_%d" % h, w2_q[0], right, "a%d" % h, halves[h]) for h in range(2)]
        for h in range(2):
            nc.scalar.copy(windows[0][:, halves[h]], e0[h][:])
        for h in range(2):
            round_half(nc.scalar.copy, w1_grouped, w1_raw, h)
        for t, bank in ((1, "a2"), (2, "a3"), (LAST, "a2")):
            nc.scalar.copy(windows[t][:, :S], project("e%d" % t, w2_q[t], right, bank)[:])
        gather_first(0, halves)
        for cols in halves:
            gather_less_first(third[0][:, cols], 0, c3_list, cols)
        w1_q = quantise("w1_low", w1_grouped[:, 0:2]) + quantise("w1_high", w1_grouped[:, 2:4])
        y = [project("y%d" % t, w1_q[t], left, "y%d" % t) for t in range(TILES)]
        gather_first(1, [whole])
        times_y(half_gap[0], third[0], 0, 0.125)
        eighth_y = {t: row("eighth_y%d" % t) for t in (1, 2)}
        last_quarter_y = row("last_quarter_y")
        for t in (1, 2):
            nc.scalar.activation(eighth_y[t][:], y[t][:], ACT.Copy, scale=0.125)
        shape(0, "a0")
        nc.scalar.activation(last_quarter_y[:], y[LAST][:], ACT.Copy, scale=0.25)
        gather_less_first(third[1][:], 1, c3_list)
        nc.gpsimd.tensor_tensor(half_gap[1][:], third[1][:], eighth_y[1][:], ALU.mult)
        gather_first(2, halves)
        shape(1, "a1")
        for cols in halves:
            gather_less_first(third[2][:, cols], 2, c3_list, cols)
        nc.gpsimd.tensor_tensor(half_gap[2][:], third[2][:], eighth_y[2][:], ALU.mult)
        first[LAST] = row("first3", tag="third1")
        gather_first(LAST, halves)
        for cols in halves:
            nc.scalar.activation(size[2][:, cols], half_gap[2][:, cols], ACT.Abs)
        for cols in halves:
            nc.scalar.activation(small[:, small_at[2]][:, cols], size[2][:, cols], ACT.Exp, scale=-2.0)
        open_lead(2, "a3")
        last_third = [row("third3_0", HALF, tag="second"), row("third3_1", HALF)]
        for h, cols in enumerate(halves):
            gather_less_first(last_third[h][:], LAST, c3_list, cols)
        slope[LAST] = row("slope3")
        for h, cols in enumerate(halves):
            nc.vector.scalar_tensor_tensor(
                last_gap[:, cols], last_third[h][:], 0.25, y[LAST][:, cols], ALU.mult, ALU.mult
            )
            nc.scalar.activation(slope[LAST][:, cols], last_gap[:, cols], ACT.Tanh, scale=0.5)
        for h, cols in enumerate(halves):
            nc.scalar.activation(blocks(small[:], last_at[h]), blocks(slope[LAST][:, cols]), ACT.Abs)

        second = keep.tile([P, TILES, S], F32, name="second", tag="second", align_bytes=64)
        s12 = [row("s12_%d" % t) for t in range(LAST)]
        last_s21 = row("last_s21")
        soft = row("soft", TILES * S)
        for run in (slice(0, 2 * S), slice(2 * S, 4 * S)):
            nc.scalar.activation(soft[:, run], small[:, run], ACT.Ln, bias=1.0)
        for cols in halves:
            gather_less_first(second[:, 0, cols], 0, c2_list, cols)
        gather_less_first(second[:, 1, :], 1, c2_list)
        times_y(s12[0], second[:, 0, :], 0, -0.25)
        for t in (2, LAST):
            gather_less_first(second[:, t, :], t, c2_list)
        nc.gpsimd.tensor_tensor(last_s21[:], second[:, LAST, :], last_quarter_y[:], ALU.mult)
        times_y(s12[1], second[:, 1, :], 1, -0.25)
        for cols in halves:
            times_y(s12[2], second[:, 2, :], 2, -0.25, cols)
        last_top = [row("last_top%d" % h, HALF) for h in range(2)]
        last_lead = [row("last_lead%d" % h, HALF) for h in range(2)]
        for h, cols in enumerate(halves):
            nc.vector.scalar_tensor_tensor(
                blocks(last_top[h][:]), blocks(last_gap[:, cols]), 0.0, blocks(soft[:], last_at[h]),
                ALU.max, ALU.subtract,
            )
        for h, cols in enumerate(halves):
            nc.vector.tensor_tensor(last_lead[h][:], last_top[h][:], last_s21[:, cols], ALU.subtract)
        turn(lead[0][:], s12[0][:])
        turn(lead[0][:], soft[:, small_at[0]], closes=True)
        for t in (1, 2):
            turn(lead[t][:], soft[:, small_at[t]])
        for t in (1, 2):
            turn(lead[t][:], s12[t][:], closes=True)

        turned = [(n // 2, n % 2) for n in range(2 * LAST)]
        pieces = turned + [(LAST, h) for h in range(2)]
        outer = []
        for n, bank in enumerate(("y0", "y1", "y3", "a2", "a0", "y2")):
            t, h = turned[n]
            outer_turned = row("outer_turned%d" % n, HALF)
            nc.scalar.activation(outer_turned[:], lead[t][:, halves[h]], ACT.Tanh, scale=0.5)
            outer.append(psum.tile([P, HALF], F32, name="outer%d" % n, tag=bank))
            turn(outer[n][:], outer_turned[:], opens=True, closes=True)
        slope[2] = row("slope2", tag="outer_turned0")
        nc.scalar.activation(slope[2][:], half_gap[2][:], ACT.Tanh)
        for h in range(2):
            outer.append(row("last_outer%d" % h, HALF))
            nc.scalar.activation(outer[-1][:], last_lead[h][:], ACT.Tanh, bias=0.5 * math.log(2.0), scale=0.5)
        shift = [row("shift0", HALF, tag="last_top0")] + [row("shift%d" % n, HALF) for n in range(1, len(pieces))]
        for n, (t, h) in enumerate(pieces):
            nc.vector.scalar_tensor_tensor(shift[n][:], outer[n][:], 1.0, slope[t][:, halves[h]], ALU.add, ALU.mult)
        rows = out.rearrange("(p t) j -> p t j", t=TILES)
        for n, (t, h) in enumerate(pieces):
            result = row("result%d" % n, HALF, tag="last_lead1" if n == GPSIMD_HALVES else None)
            if n < GPSIMD_HALVES:
                nc.gpsimd.tensor_scalar(result[:], shift[n][:], 0.5, 1.0, ALU.mult, ALU.add)
            elif t < LAST:
                nc.scalar.activation(result[:], shift[n][:], ACT.Identity, bias=1.0, scale=0.5)
            else:
                nc.vector.tensor_scalar(result[:], shift[n][:], 0.5, 1.0, ALU.mult, ALU.add)
            nc.sync.dma_start(rows[:, t, halves[h]], result[:])
